import numpy as np, ml_dtypes
CORES = [48,51,52,55]
N = 4
BF = ml_dtypes.bfloat16
V, X, PS, RO, EP = 2048, 512, 128, 3, 2
K = V // PS; W = V + (N - 1) * X
def blocks(a):
    return np.repeat(np.swapaxes(a, -1, -2), PS, axis=-1)
def kin(rng):
    sh = (N, 8, 16, V); u = rng.random(sh)
    a = blocks(rng.integers(0, K, (8, K, 16))) * PS + rng.integers(0, PS, sh)
    return np.where(u > 0.95, np.arange(V), np.where(u < 0.5, a, rng.integers(0, W, sh)))
def parts(rng):
    sh = (N, 8, 16, V)
    p = rng.choice(np.array([0.3, 0.6, 0.8, 0.95]), (8, K, 16))
    s = np.maximum(rng.integers(40, 256, (8, K, 16)) * rng.choice(np.array([0.25, 0.5, 1.0]), (N, 8, K, 16)), 1.0)
    w = np.where(rng.random(sh) < blocks(p), 1 + (rng.random(sh) * blocks(s)).astype(np.int64), 0)
    l = kin(rng); r = kin(rng)
    same = rng.random((8, K)) < 0.25; same[np.arange(8), rng.integers(0, K, 8)] = True
    r = np.where(np.repeat(same, PS, axis=1)[:, None, :], l, r)
    return w, l, r
def pack(w, l, r):
    return {"w": np.ascontiguousarray(w).reshape(N, 128, V).astype(np.float32).astype(BF), "kids": np.ascontiguousarray(l + 4096 * r).reshape(N, 128, V).astype(np.int32)}
def setup_inputs(rng):
    w, l, r = parts(rng)
    return pack(w, l, r)
KL = np.array([1, 2, 6, 4, 5, 6, 6, 7, 6, 9, 11, 11, 13, 14, 12, 11])
KR = np.array([1, 2, 6, 4, 5, 7, 6, 7, 8, 9, 12, 11, 13, 14, 12, 6])
HQ = np.array([100, 100, 100, 100, 100, 100, 100, 60, 60, 0, 120, 20, 100, 100, 100, 120])
def crypt(rng, w, l, r, g):
    ops = [int(i) for i in 1 + rng.permutation(15)[:5]]; q, p, u = ops[:3]
    z = 2 * PS; h = PS // 4; cp = h // 8; s = z + 2 * h; e = z + PS
    w[:, g, :, z:e] = 0; w[:, g, p, z:z + h] = 255
    nul = z + h + rng.integers(0, h, (N, 1, h)); l[:, g, :, z:z + h] = nul; r[:, g, :, z:z + h] = nul
    at = s + np.arange(16)[:, None] * cp + np.arange(cp)
    l[:, g, :, s:e] = at[KL].reshape(-1); r[:, g, :, s:e] = at[KR].reshape(-1)
    w[:, g, q, s:e] = np.repeat(HQ, cp)
    w[:, g, 0, s + 9 * cp:s + 10 * cp] = 100; w[:, g, u, s + 6 * cp:s + 7 * cp] = 50
    return at, ops
def seat(rng, w, l, r, g, k, ops, x, y):
    e = slice(k * PS, k * PS + PS); q, u = ops[0], ops[2]
    w[:, g, :, e] = rng.integers(0, 51, (N, 16, PS)); w[:, g, 0, e] = 0; w[:, g, u, e] = 0
    w[:, g, q, e] = rng.integers(200, 256, (N, PS)); l[:, g, q, e] = x; r[:, g, q, e] = y
def lone(rng, w, l, r, g, n):
    at, ops = crypt(rng, w, l, r, g); cp = at.shape[1]; bl = [k for k in range(K) if k != 2]
    for j in range(N + 1):
        m = rng.random((N, PS)) < 0.5
        if j < N:
            m = np.zeros((N, PS), bool); m[j, rng.integers(0, PS)] = True
        x = at[3 - n + 3 * m, rng.integers(0, cp, (N, PS))]
        seat(rng, w, l, r, g, bl[j], ops, x, x)
def stage(rng, w, l, r, g):
    at, ops = crypt(rng, w, l, r, g); cp = at.shape[1]; q, p, u, a, b = ops; sh = (N, PS)
    def some(j):
        return at[j, rng.integers(0, cp, sh)]
    y = some(6); w[:, g, :, :PS] = 0; w[:, g, u, :PS] = rng.integers(200, 256, sh); l[:, g, u, :PS] = y; r[:, g, u, :PS] = y
    x = some(8); seat(rng, w, l, r, g, 1, ops, x, x)
    x = some(9); seat(rng, w, l, r, g, 3, ops, x, x)
    m = np.argsort(rng.random(sh), axis=1) < 5 * PS // 8; i = rng.integers(0, cp, sh)
    seat(rng, w, l, r, g, 4, ops, at[np.where(m, 14, 10), i], at[np.where(m, 11, 12), i])
    seat(rng, w, l, r, g, 5, ops, some(15), some(12))
    x = V + rng.integers(0, N - 1, sh) * X + rng.integers(0, PS, sh); seat(rng, w, l, r, g, 6, ops, x, x)
    x = some(6); seat(rng, w, l, r, g, 7, ops, x, x + V)
    x = some(6); seat(rng, w, l, r, g, 8, ops, x, x + 2048)
    e = slice(9 * PS, 10 * PS); lo, hi = min(a, b), max(a, b); x = some(6); y = some(7)
    seat(rng, w, l, r, g, 9, ops, x, x); w[:, g, q, e] = rng.integers(100, 150, sh)
    v = rng.integers(150, 255, N * PS); v[0] ^= np.add.reduce(v) & 1
    o = rng.permutation(v); o[np.argmin(o)] += 1
    w[:, g, lo, e] = v.reshape(sh); w[:, g, hi, e] = o.reshape(sh)
    l[:, g, lo, e] = x; r[:, g, lo, e] = x; l[:, g, hi, e] = y; r[:, g, hi, e] = y
def setup_inputs_twin(rng):
    w, l, r = parts(rng); P = PS
    w[:, :2, :, :P] = 255
    w[:, :2, :, P:2 * P] = rng.integers(200, 256, (N, 2, 16, P))
    w[:, :2, :, 2 * P:3 * P] = rng.integers(100, 151, (N, 2, 16, P))
    w[:, :2, :, 3 * P:4 * P] = np.where(rng.random((N, 2, 16, P)) < 0.6, rng.integers(1, 10, (N, 2, 16, P)), 0)
    c = 2 * P + rng.integers(0, P, (N, 2, 1, P))
    l[:, :2, :, :P] = c; r[:, :2, :, :P] = P + np.arange(P)
    l[:, :2, :, P:2 * P] = 3 * P + rng.integers(0, P, (N, 2, 16, P)); r[:, :2, :, P:2 * P] = c
    l[:, :2, :, 2 * P:3 * P] = 3 * P + rng.integers(0, P, (N, 2, 16, P)); r[:, :2, :, 2 * P:3 * P] = 3 * P + rng.integers(0, P, (N, 2, 16, P))
    odd = np.arange(1, K, 2) * P + P - 1
    big = w[N - 1, 4:6]; big[:, :, odd] = 255
    r[:, 4:7] = np.where(w[:, 4:7] == 0, rng.integers(0, W, (N, 3, 16, V)), l[:, 4:7])
    sub = r[N - 1, 4:6]; sub[:, :, odd] = (l[N - 1, 4:6][:, :, odd] + 1) % W
    lone(rng, w, l, r, 2, 1); stage(rng, w, l, r, 3); lone(rng, w, l, r, 7, RO - 1)
    return pack(w, l, r)
def setup_inputs_ties(rng):
    w, l, r = parts(rng); h = (K // 2) * PS
    w[:, 0] = 255
    w[:, 1] = np.where(w[:, 1] > 0, 9, 0)
    for g in (1, 4, 5): w[:, g, 1::2] = w[:, g, 0::2]
    w[:, 6] = np.minimum(w[:, 6], 2)
    w[:, 2:4, :, :h] = 255
    a = h + rng.integers(0, V - h, (N, 2, 16, h)); l[:, 2:4, :, :h] = a
    r[:, 2:4, :, :h] = a.reshape(N, 2, 16, K // 2, PS)[..., rng.permutation(PS)].reshape(N, 2, 16, h)
    e = (K - 2) * PS; f = (K - 1) * PS
    w[:, 7, :, :2 * PS] = 255; w[:, 7, :, e:] = 0
    w[:, 7, 9, e:f] = 100; w[:, 7, 2, f:] = 100
    l[:, 7, :, :2 * PS] = e + rng.integers(0, PS, (N, 16, 2 * PS)); r[:, 7, :, :2 * PS] = f + rng.integers(0, PS, (N, 16, 2 * PS))
    l[:, 7, :, e:f] = f + rng.integers(0, PS, (N, 16, PS)); r[:, 7, :, e:f] = f + rng.integers(0, PS, (N, 16, PS))
    l[:, 7, :, f:] = e + rng.integers(0, PS, (N, 16, PS)); r[:, 7, :, f:] = e + rng.integers(0, PS, (N, 16, PS))
    return pack(w, l, r)
def setup_inputs_scarce(rng):
    w, l, r = parts(rng); q = rng.permutation(N)
    w = np.where(rng.random(w.shape) < blocks(rng.choice(np.array([0.1, 0.3, 0.6]), (8, K, 16))), w, 0)
    w[q[0], 4:] = 0; w[:, 0, :, :PS] = 0
    w[:, 1, :, 2 * PS:3 * PS] = 0; v = 2 * PS + 5
    w[q[1], 1, :, v] = 255; l[q[1], 1, :, v] = V; r[q[1], 1, :, v] = W - 1
    w[:, 1, :, 0] = 200; w[:, 1, :, X - 1] = 100
    return pack(w, l, r)
def setup_inputs_ends(rng):
    w, l, r = parts(rng); e = np.array([0, V - 1, V, W - 1, X - 1])
    for g in (0, 3, 6):
        l[:, g] = rng.choice(e, (N, 16, V)); r[:, g] = rng.choice(e, (N, 16, V))
    for g in (1, 5): l[:, g] = np.where(rng.random((N, 1, V)) < 0.4, np.arange(V), l[:, g])
    l[:, 2] = rng.integers(V, W, (N, 16, V)); r[:, 2] = rng.integers(V, W, (N, 16, V)); w[:, 2] = np.maximum(w[:, 2], 1)
    l[:, 4] = rng.integers(0, V, (N, 16, V)); r[:, 4] = rng.integers(0, V, (N, 16, V))
    r[:, 7] = np.where(rng.random((N, 16, V)) < 0.5, np.arange(V), r[:, 7])
    return pack(w, l, r)
def setup_inputs_spread(rng):
    w, l, r = parts(rng); sh = w.shape
    w = np.minimum((np.exp2(8 * rng.random((N, 8, 1, V))) * rng.random(sh)).astype(np.int64), 255)
    l = np.where(rng.random(sh) < 0.5, np.minimum((W * rng.random(sh) ** 3).astype(np.int64), W - 1), l)
    return pack(w, l, r)
def check_inputs(d):
    bad = []; v = d["w"].astype(np.float32); k = d["kids"].astype(np.int64)
    if not np.all((v >= 0) & (v <= 255) & (v == np.floor(v))): bad.append("whole numbers of w")
    if np.min(k) < 0 or np.max(k & 4095) >= W or np.max(k >> 12) >= W: bad.append("class numbers of kids")
    return bad
def pick(tab, o, c):
    return np.take_along_axis(tab.reshape(N, 8, 16 * W), o * W + c, 2)
def reference(w, kids):
    tw = w.astype(np.float32).astype(np.int64).reshape(N, 8, 16, V); kd = kids.astype(np.int64).reshape(N, 8, 16, V)
    tl = kd & 4095; tr = kd >> 12; own = np.arange(V)
    ghost = np.broadcast_to(np.arange(V, W), (N, 8, 16, W - V))
    for ep in range(EP):
        fw = np.stack([np.concatenate([tw[a]] + [tw[(a - d) % N][:, :, :X] for d in range(1, N)], axis=2) for a in range(N)])
        fl = np.concatenate([tl, ghost], axis=3); fr = np.concatenate([tr, ghost], axis=3)
        live = np.ones((N, 8, V), bool); b = np.zeros((RO + 1, N, 8, V), np.int64); b[0] = own
        have = np.zeros((RO + 1, 8, K), bool); have[0] = True; x = []
        for t in range(1, RO + 1):
            U = np.zeros((8, K, t, 16), np.int64)
            for h in range(t):
                m = np.minimum(np.take_along_axis(fw, b[h][:, :, None, :], 3), tw) * live[:, :, None, :]
                s = np.add.reduce(np.add.reduce(m.reshape(N, 8, 16, K, PS), axis=4), axis=0)
                U[:, :, h] = np.where(have[h][:, :, None], s.transpose(0, 2, 1), -1)
            best = np.argmax(U.reshape(8, K, t * 16), axis=2)
            bh = np.repeat(best >> 4, PS, axis=1); bo = np.repeat(best & 15, PS, axis=1)
            cur = np.take_along_axis(b, np.broadcast_to(bh, (1, N, 8, V)), 0)[0]; x.append(cur)
            live = live & (pick(fw, bo, cur) > 0)
            lk = pick(fl, bo, cur); rk = pick(fr, bo, cur)
            b = np.where(np.arange(RO + 1)[:, None, None, None] == bh, lk, b); b[t] = rk
            drop = np.zeros((8, K), bool)
            for h in range(t):
                differ = np.any((live & (rk != b[h])).reshape(N, 8, K, PS), axis=(0, 3))
                drop = drop | (have[h] & ~differ)
            have[t] = ~drop
        lf = np.concatenate([live, np.zeros((N, 8, W - V), bool)], axis=2); die = np.zeros((N, 8, V), bool)
        for c in x[1:]: die = die | (np.take_along_axis(lf, c, 2) & (c != own))
        go = (live & ~die)[:, :, None, :]
        h0 = b[0]; h1 = b[0]
        for t in range(RO, 0, -1): h1 = np.where(np.repeat(have[t], PS, axis=1), b[t], h1)
        h0 = h0[:, :, None, :]; h1 = h1[:, :, None, :]
        nw = (np.take_along_axis(fw, h0, 3) + np.take_along_axis(fw, h1, 3)) >> 1
        tw = np.where(go, nw, tw); tl = np.where(go, h0, tl); tr = np.where(go, h1, tr)
    return {"yw": tw.reshape(N, 128, V).astype(np.float32).astype(BF), "yk": (tl + 4096 * tr).reshape(N, 128, V).astype(np.float32)}

@@ -1,0 +1,674 @@
+import numpy as np
+from concourse.bass import DstId, RemoteDMATransfer
+from concourse.mybir import AluOpType as ALU, AxisListType, ActivationFunctionType as ACT
+import comms_topo
+
+V, X = 2048, 512
+H = 2
+KN = 16 // H
+NP = V // H
+C = 128 // H
+NC = NP // 128
+WW = 3600
+Z = 3584
+BIG = 16777216.0
+ZV = 4097.0 * Z
+MAG = 51539607552.0
+NV2 = (8, 4)
+NV3 = (8, 8, 4)
+CP = 512
+VC = 4
+CY, PE, CG, WAKE, RLAT, DLAT, SELF = 0.83e-3, 0.6e-3, 1.56, 0.06, 2.2, 2.5, 0.06
+
+SF = 70; SU = 8; SB = 8; SC = 96
+SCRATCH = {
+    "W1": ("sbuf", [128, WW], "bfloat16"), "W2": ("sbuf", [128, WW], "bfloat16"),
+    "KT": ("sbuf", [128, WW], "float32"), "KI": ("sbuf", [128, V], "int32"),
+    "WP": ("sbuf", [128, V], "bfloat16"), "GI": ("sbuf", [128, 3 * X], "float32"), "PR": ("sbuf", [128, V], "bfloat16"),
+    "LV": ("sbuf", [128, V + 16], "bfloat16"),
+    "LR": ("sbuf", [128, 2048], "bfloat16"), "FD": ("sbuf", [128, 2048], "bfloat16"),
+    "IC": ("sbuf", [128, 128], "int32"), "ID": ("sbuf", [128, 128], "int32"), "IM": ("sbuf", [128, 128], "int32"), "IS": ("sbuf", [128, 64], "int32"),
+    "IV": ("sbuf", [128, 128], "float32"), "IP": ("sbuf", [128, 2], "int32"), "IQ": ("sbuf", [128, 4], "int32"), "PG": ("sbuf", [128, 8], "float32"), "CI": ("sbuf", [128, 16], "int32"), "CM": ("sbuf", [128, 16], "float32"),
+    "IB": ("sbuf", [128, 128], "bfloat16"), "NB": ("sbuf", [128, 128], "bfloat16"), "HB": ("sbuf", [128, 128], "bfloat16"), "NI": ("sbuf", [128, 128], "bfloat16"),
+    "BT": ("sbuf", [128, 512], "bfloat16"), "QT": ("sbuf", [128, 512], "bfloat16"),
+    "CB": ("sbuf", [128, 384], "bfloat16"), "F": ("sbuf", [128, 128], "float16"), "E": ("sbuf", [128, 128], "float16"),
+    "GQ": ("sbuf", [128, 128], "bfloat16"), "MK": ("sbuf", [128, 128], "bfloat16"), "SL": ("sbuf", [128, C], "float32"),
+    "T1": ("sbuf", [128, 128], "float32"), "T2": ("sbuf", [128, 128], "float32"), "T3": ("sbuf", [128, 128], "float32"),
+}
+for _j in range(7): SCRATCH["IT%d" % _j] = ("sbuf", [128, 128], "int32")
+for _h in range(H):
+    for _n, _w, _t in (("G", NP, "float32"), ("M0", NP, "bfloat16"), ("M1", NP, "bfloat16"), ("M2", NP, "bfloat16"), ("RW", NP, "bfloat16"),
+                       ("GA", NP, "bfloat16"), ("GB", NP, "bfloat16"), ("SND0", 392, "float16"), ("SND1", 392, "float16"), ("LND0", 3 * 392, "float16"),
+                       ("LND1", 3 * 392, "float16"), ("OH", 384, "bfloat16"), ("OT", 128, "float32"), ("XX", 128, "float32"),
+                       ("SF", SF * C, "float32"), ("SU", SU * C, "uint16"), ("SB", SB * C, "bfloat16"), ("SC", SC, "float32")):
+        SCRATCH["%s_%d" % (_n, _h)] = ("sbuf", [128, _w], _t)
+for _b in range(8):
+    SCRATCH["B%d" % _b] = ("psum", [128, 512], "float32")
+SEMAPHORES = ["cV", "cS", "cP", "cG"] + ["d%d" % i for i in range(44)] + ["a%d" % i for i in range(22)] + ["l%d" % i for i in range(22)]
+
+
+def rank_program(g, core, T, topo):
+    rank = T.rank_of(core)
+    if rank is None:
+        return
+    eng = {"V": g.vector, "S": g.scalar, "P": g.tensor, "G": g, "Y": g.sync}
+    cnt = {}; known = {q: {} for q in eng}; wr = {}; rd = {}; bank = {}; snap = {}; nd = [0, 0]
+    nodes = []
+
+    def put(d, k, s, v):
+        e = d.setdefault(k, {}); e[s] = max(e.get(s, 0), v)
+
+    def bk(k):
+        return k[0] if isinstance(k, tuple) and isinstance(k[0], int) else None
+
+    def waits(q, R, W):
+        own = "c" + q; need = {}
+        for k in R:
+            for s, v in wr.get(k, {}).items(): need[s] = max(need.get(s, 0), v)
+        for k in W:
+            for d in (wr, rd):
+                for s, v in d.get(k, {}).items():
+                    if s != own or q != "P": need[s] = max(need.get(s, 0), v)
+        for k in list(R) + list(W):
+            if bk(k) is not None:
+                for s, v in bank.get(bk(k), {}).items():
+                    if s != own: need[s] = max(need.get(s, 0), v)
+        kn = known[q]
+        for s in sorted((s for s, v in need.items() if kn.get(s, 0) < v), key=lambda s: s == own):
+            v = need[s]
+            if kn.get(s, 0) >= v: continue
+            eng[q].wait_ge(T.sem[s], v)
+            kn[s] = v
+            for s2, v2 in snap.get((s, v), {}).items(): kn[s2] = max(kn.get(s2, 0), v2)
+
+    def mark(R, W, s, v):
+        for k in R: put(rd, k, s, v)
+        for k in W: put(wr, k, s, v)
+        for k in list(R) + list(W):
+            if bk(k) is not None: put(bank, bk(k), s, v)
+
+    def done(q, R, W, i):
+        s = "c" + q; cnt[s] = cnt.get(s, 0) + 1
+        i.then_inc(T.sem[s], 1)
+        snap[(s, cnt[s])] = dict(known[q])
+        mark(R, W, s, cnt[s])
+
+    def node(q, R, W, emit, cost, lat=0.0):
+        nodes.append([q, list(R), list(W), emit, cost, lat])
+
+    def op(q, R, W, make, n=64, cy=1.0):
+        cost = 0.06 + max(64, n * cy) * CY if q != "P" else cy * max(64, n) * PE
+        R = list(R); W = list(W)
+
+        def emit(q):
+            waits(q, R, W)
+            done(q, R, W, make(eng[q], q))
+        node(q, R, W, emit, cost)
+
+    def dma(q, R, W, out, in_):
+        s = "d%d" % nd[0]; nd[0] += 1
+
+        def emit(q):
+            waits(q, R, W)
+            eng[q].dma_start(out, in_).then_inc(T.sem[s], 16)
+            cnt[s] = 16; snap[(s, 16)] = dict(known[q]); mark(R, W, s, 16)
+        node(q, R, W, emit, 0.06, DLAT)
+
+    peers = [T.cores[(rank + d) % 4] for d in (1, 2, 3)]
+    ids = []; mask = 0xFFFF
+    for p in peers:
+        rid, pid = topo.addr(p)[:2]
+        ids.append(DstId(rid=rid, pnc=pid)); mask &= topo.mask(core, p)
+
+    def send(R, W, src, dsts):
+        a, l = "a%d" % nd[1], "l%d" % nd[1]; nd[1] += 1
+        n = bin(mask).count("1")
+
+        def emit(q):
+            waits("G", R, ())
+            g.remote_dma_fused([RemoteDMATransfer(dst_ids=ids, dma_engine_mask=mask, remote_sem=T.sem[a], srcs=[src], dsts=dsts)], local_sem=T.sem[l])
+            cnt[a] = 3 * n; cnt[l] = n
+            mark(R, (), l, n); snap[(l, n)] = dict(known["G"])
+            for k in W: wr[k] = {a: 3 * n}
+        node("G", R, W, emit, 0.6, RLAT)
+
+    def ts(R, W, o, i, s1, op0, s2=None, op1=None, n=64, cy=1.0):
+        if op1 is None: op("V", R, W, lambda e, q: e.tensor_scalar(o, i, s1, None, op0), n, cy)
+        else: op("V", R, W, lambda e, q: e.tensor_scalar(o, i, s1, s2, op0, op1), n, cy)
+
+    def tt(R, W, o, a, b, f, n=64, cy=2.0): op("V", R, W, lambda e, q: e.tensor_tensor(o, a, b, f), n, cy)
+    def red(R, W, o, i, n=64): op("V", R, W, lambda e, q: e.tensor_reduce(o, i, AxisListType.X, ALU.max), n)
+    def vcopy(R, W, o, i, n=64): op("V", R, W, lambda e, q: e.tensor_copy(o, i), n)
+    def fill(W, o, c, n=64): op("V", (), W, lambda e, q: e.memset(o, c), n)
+    def mm(R, W, o, l, r, st=True, sp=True, n=128, cy=1.0): op("P", R, W, lambda e, q: e.matmul(o, l, r, st, sp), n, cy)
+    def act(R, W, o, i, f=ACT.Copy, n=64, cy=1.0, **kw): op("S", R, W, lambda e, q: e.activation(o, i, f, **kw), n, cy)
+
+    def iota(W, o, pat, base, ch, n, **kw): op("G", (), W, lambda e, q: e.iota(o, pat, base, ch, **kw), 2 * n)
+
+    def cp(R, W, o, i, n, cy=1.0): op("VS", R, W, lambda e, q: e.tensor_copy(o, i) if q == "V" else e.activation(o, i, ACT.Copy), n, cy)
+
+    def lin(R, W, o, i, scale, bias=None, n=64):
+        def make(e, q):
+            if bias is None: return e.tensor_scalar(o, i, scale, None, ALU.mult) if q == "V" else e.activation(o, i, ACT.Copy, scale=scale)
+            return e.tensor_scalar(o, i, scale, bias, ALU.mult, ALU.add) if q == "V" else e.activation(o, i, ACT.Identity, scale=scale, bias=bias)
+        op("VS", R, W, make, n)
+
+    def hot(R, W, o, i, bias, n):
+        op("VS", R, W, lambda e, q: e.tensor_scalar(o, i, bias, 0.0, ALU.add, ALU.max) if q == "V" else e.activation(o, i, ACT.Relu, bias=bias), n)
+    B = [T["B%d" % b] for b in range(8)]
+    slot = {}
+
+    def arr(kind, h, name):
+        d = slot.setdefault((kind, h), {})
+        if name not in d: d[name] = len(d)
+        w = 1 if kind == "SC" else C
+        j = d[name] * w
+        return T["%s_%d" % (kind, h)][:, j:j + w]
+
+    def view(kind, h):
+        return (lambda n: arr(kind, h, n)), (lambda n: (kind, h, n))
+
+    for b in range(4):
+        dma("Y", (), [("w", 1, b)], T.W1[:, 512 * b:512 * b + 512], T.w[:, 512 * b:512 * b + 512])
+    for b in range(4):
+        dma("S", (), [("ki", b)], T.KI[:, 512 * b:512 * b + 512], T.kids[:, 512 * b:512 * b + 512])
+    iota(["IC"], T.IC[:], [[1, 128]], 0, 0, 128)
+    iota(["ID"], T.ID[:], [[1, 128]], 128, -1, 128)
+    iota(["IP"], T.IP[:, 0:2], [[0, 2]], 0, 1, 32)
+
+    def ghosts(ep):
+        t = T["W%d" % ep]
+        send([("w", ep, 0)], [("wg", ep)], t[:, 0:X], [t[:, V + (d - 1) * X:V + d * X] for d in (1, 2, 3)])
+    ghosts(1)
+    iota(["IM"], T.IM[:], [[1, 128]], 0, KN, 128)
+    iota(["IS"], T.IS[:, 0:C], [[-H, C]], 0, 1, C)
+    iota(["CI"], T.CI[:], [[1, 16]], 0, 0, 32)
+    iota(["GI"], T.GI[:], [[4097, 3 * X]], V * 4097, 0, 3 * X, allow_small_or_imprecise_dtypes=True)
+
+    LH = {1: 0, 2: 1, 4: 2}[H]; LK = 4 - LH
+    IT = [T["IT%d" % j] for j in range(7)]
+    ts(["ID"], ["IB"], T.IB[:], T.ID[:], 128.0, ALU.is_equal, n=128)
+    fill(["BT"], T.BT[:], BIG, n=256)
+    lin(["IB"], ["NB"], T.NB[:], T.IB[:], -BIG, n=128)
+    ts(["ID"], ["IT0"], IT[0][:], T.ID[:], KN - 1, ALU.bitwise_and, n=128)
+    ts(["IT0"], ["F"], T.F[:], IT[0][:], 0.0, ALU.is_equal, 64.0, ALU.mult, n=128)
+    ts(["IP"], ["IQ0"], T.IQ[:, 0:1], T.IP[:, 0:1], 4, ALU.arith_shift_right)
+    ts(["IP"], ["IQ1"], T.IQ[:, 1:2], T.IP[:, 1:2], 15, ALU.bitwise_and)
+    vcopy(["IQ0", "IQ1"], ["PG"], T.PG[:, 0:2], T.IQ[:, 0:2])
+    ts(["IC"], ["IT1"], IT[1][:], T.IC[:], 4, ALU.arith_shift_right, n=128)
+    ts(["IT1", "PG"], ["GQ"], T.GQ[:], IT[1][:], T.PG[:, 0:1], ALU.is_equal, n=128)
+    lin(["GQ"], ["T1"], T.T1[:], T.GQ[:], BIG, -BIG, n=128)
+    ts(["IC"], ["IT2"], IT[2][:], T.IC[:], 15, ALU.bitwise_and, n=128)
+    ts(["IT2"], ["T2"], T.T2[:], IT[2][:], -1.0, ALU.mult, 15.0, ALU.add, n=128)
+    for s in range(3): tt(["T1", "T2"], [("CB", s)], T.CB[:, 128 * s:128 * s + 128], T.T1[:], T.T2[:], ALU.add, n=128)
+    CBK = [("CB", 0), ("CB", 1), ("CB", 2)]
+    ts(["IM"], ["IT3"], IT[3][:], T.IM[:], LK, ALU.arith_shift_right, H - 1, ALU.bitwise_and, n=128)
+    ts(["IT3"], ["MK"], T.MK[:], IT[3][:], 0.0, ALU.is_equal, n=128)
+    ts(["IS"], ["IT4"], IT[4][:, 0:C], T.IS[:, 0:C], LH, ALU.arith_shift_right)
+    ts(["IT4"], ["SL"], T.SL[:], IT[4][:, 0:C], 0.0, ALU.is_equal)
+    lin(["IB"], ["NI"], T.NI[:], T.IB[:], -1.0, n=128)
+    ts(["F"], ["T3"], T.T3[:], T.F[:], 1.0 / 64, ALU.mult, n=128)
+    tt(["T3", "GQ"], ["E"], T.E[:], T.T3[:], T.GQ[:], ALU.mult, n=128)
+    for ep in (1, 2): fill([("wz", ep)], T["W%d" % ep][:, Z:WW], 0.0)
+    fill(["ktz"], T.KT[:, Z:WW], BIG)
+    ts(["IQ1"], ["IQ2"], T.IQ[:, 2:3], T.IQ[:, 1:2], KN - 1, ALU.bitwise_and)
+    ts(["IQ1"], ["IQ3"], T.IQ[:, 3:4], T.IQ[:, 1:2], LK, ALU.arith_shift_right)
+    ts(["IQ2"], ["PG2"], T.PG[:, 2:3], T.IQ[:, 2:3], 128.0, ALU.mult)
+    tt(["PG2", "IQ3"], ["PG3"], T.PG[:, 3:4], T.PG[:, 2:3], T.IQ[:, 3:4], ALU.add)
+    for h in range(H):
+        ts(["IC"], [("IT", 5 + h)], IT[5 + h][:, 0:C], T.IC[:, 0:C], float(H), ALU.mult, float(h * KN * 128), ALU.add)
+        ts([("IT", 5 + h), "PG3"], [("IV", h)], T.IV[:, C * h:C * h + C], IT[5 + h][:, 0:C], T.PG[:, 3:4], ALU.add)
+    ts(["CI", "PG"], ["CM"], T.CM[:], T.CI[:], T.PG[:, 1:2], ALU.is_equal)
+    fill([("lvz",)], T.LV[:, V:V + 16], 0.0)
+    fill(["QT"], T.QT[:], -0.25, n=256)
+    lin(["IB"], ["HB"], T.HB[:], T.IB[:], 0.5, n=128)
+    for h in range(H):
+        sc, sk = view("SC", h)
+        slot[("SC", h)] = {("D%d" % n): n for n in range(8)}
+        for n in ("k0", "k1", "r0", "r1", "r2", "c0", "c1", "c2", "sA", "sB", "sC", "z0", "z1", "z2", "z3", "v0", "v1", "v2", "y0", "y1", "y2", "b0", "b1", "b2", "q0", "q1", "q2"): sc(n)
+        fill([sk("D%d" % n) for n in range(8)], T["SC_%d" % h][:, 0:8], 0.0)
+        fill([sk("k0")], sc("k0"), 16.0)
+        fill([sk("v0")], sc("v0"), 1.0)
+    for i in range(16):
+        act(["GQ", "CM"], [("LR", i)], T.LR[:, 128 * i:128 * i + 128], T.GQ[:], scale=T.CM[:, i:i + 1], n=128)
+    for i in range(16):
+        act(["IB", "CM"], [("FD", i)], T.FD[:, 128 * i:128 * i + 128], T.IB[:], scale=T.CM[:, i:i + 1], n=128)
+
+    def positions(ep, h):
+        t = T["W%d" % ep]
+        for b in range(NP // 512):
+            P = (2 if h else 6) + b if H == 2 else 4 + b
+            n = 512 // KN
+            for k in range(KN):
+                cl = (h * KN + k)
+                mm(["IB", ("w", ep, cl // 4)], [(P, "wp")], B[P][:, k:512:KN], T.IB[:], t[:, 128 * cl + n * b:128 * cl + n * b + n], n=n)
+            cp([(P, "wp")], [("WP", h, b)], T.WP[:, h * NP + 512 * b:h * NP + 512 * b + 512], B[P][:], 512)
+
+    par = [0] * H
+
+    def ship(h, lo, hi):
+        p = par[h]
+        ln = T["LND%d_%d" % (p, h)]
+        send(([("SD", h, p)] if lo == 0 else []) + ([("SV", h, p)] if hi > 8 else []), [("LD", h, p)], T["SND%d_%d" % (p, h)][:, lo:hi], [ln[:, 392 * d + lo:392 * d + hi] for d in range(3)])
+
+    def counts(h):
+        p = par[h]
+        vcopy([("SC", h, "D%d" % n) for n in range(8)], [("SD", h, p)], T["SND%d_%d" % (p, h)][:, 0:8], T["SC_%d" % h][:, 0:8])
+
+    def vote_out(h, ns):
+        p = par[h]
+        vcopy([(h, "o1")], [("SV", h, p)], T["SND%d_%d" % (p, h)][:, 8:8 + 128 * ns], B[h][:, 0:128 * ns], n=128 * ns)
+        ship(h, 0 if ns > 1 else 8, 8 + 128 * ns)
+
+    def stage1(h, s, src, key, c, st, sp, rhs="IB"):
+        mm([rhs] + key, [(h, "o1")], B[h][:, 128 * s:128 * s + 128], src[:, 128 * c:128 * c + 128], T[rhs][:], st, sp)
+
+    def vote1(h):
+        w = T.WP[:, h * NP:h * NP + NP]
+        for c in range(NC): stage1(h, 0, w, [("WP", h, c // 4)], c, c == 0, c == NC - 1)
+        vote_out(h, 1)
+
+    def vgather(R, W, m, win, l, w, n): op("V", R, W, lambda e, q: e.tensor_tensor(m, win.indirect(l), w, ALU.min), n, CG)
+
+    def votes(ep, h, lists, nv):
+        win = T["W%d" % ep][:, 0:WW]
+        wk = [("w", ep, b) for b in range(4)] + [("wg", ep), ("wz", ep)]
+        wp = T.WP[:, h * NP:h * NP + NP]
+        for s, (l, lk) in enumerate(lists):
+            n = nv[s]; m = T["M%d_%d" % (s, h)]; rw = T["RW_%d" % h]
+            for c in range(n, NC, 4):
+                e = min(c + 4, NC); k = 128 * (e - c)
+                act(wk + [lk], [("RW", h, c)], rw[:, 128 * c:128 * e], win.indirect(l[:, 8 * c:8 * e]), n=k, cy=CG)
+                P = 6 + h
+                mm(["IB"] + [("WP", h, j) for j in sorted({c // 4, (e - 1) // 4})], [(P, "df")], B[P][:, 0:k], T.IB[:], wp[:, 128 * c:128 * e], True, False, n=k)
+                mm(["NI", ("RW", h, c)], [(P, "df")], B[P][:, 0:k], T.NI[:], rw[:, 128 * c:128 * e], False, True, n=k)
+                act([(P, "df")], [("M", h, s, j) for j in range(c, e)], m[:, 128 * c:128 * e], B[P][:, 0:k], ACT.Relu, n=k)
+            for c in range(0, n, VC):
+                e = min(c + VC, n)
+                vgather(wk + [lk] + [("WP", h, j) for j in sorted({c // 4, (e - 1) // 4})], [("M", h, s, j) for j in range(c, e)],
+                        m[:, 128 * c:128 * e], win, l[:, 8 * c:8 * e], wp[:, 128 * c:128 * e], 128 * (e - c))
+            todo = [(wp, [("WP", h, c // 4)], c, "IB") for c in range(n, NC)] + [(m, [("M", h, s, c)], c, "IB") for c in range(n)] \
+                + [(m, [("M", h, s, c)], c, "NI") for c in range(n, NC)]
+            for j, (src, key, c, r) in enumerate(todo): stage1(h, s, src, key, c, j == 0, j == len(todo) - 1, r)
+
+    def dsum(h, o, p):
+        ln = T["LND%d_%d" % (p, h)]
+        mm(["E", ("SD", h, p)], [(o, "d")], B[o][:, 384:392], T.E[:], T["SND%d_%d" % (p, h)][:, 0:8], True, False, n=8)
+        for d in range(3): mm(["E", ("LD", h, p)], [(o, "d")], B[o][:, 384:392], T.E[:], ln[:, 392 * d:392 * d + 8], False, d == 2, n=8)
+
+    def stage2(h, ns):
+        p = par[h]; par[h] = 1 - p
+        ln = T["LND%d_%d" % (p, h)]; sn = T["SND%d_%d" % (p, h)]
+        o = 2 + h; w = 128 * ns
+        if ns > 1: dsum(h, 4 + h, p)
+        mm(CBK + ["IB"], [(o, "o2")], B[o][:, 0:w], T.IB[:], T.CB[:, 0:w], True, False, n=w)
+        mm(["F", ("SV", h, p)], [(o, "o2")], B[o][:, 0:w], T.F[:], sn[:, 8:8 + w], False, False, n=w)
+        for d in range(3): mm(["F", ("LD", h, p)], [(o, "o2")], B[o][:, 0:w], T.F[:], ln[:, 392 * d + 8:392 * d + 8 + w], False, d == 2, n=w)
+
+    def onehot(h, ns):
+        oh = T["OH_%d" % h]; b = 4 + h
+        for s in range(ns): mm([("OH", h, s), "IB"], [(b, "ot")], B[b][:, 0:128], oh[:, 128 * s:128 * s + 128], T.IB[:], s == 0, s == ns - 1)
+        cp([(b, "ot")], [("OT", h)], T["OT_%d" % h][:], B[b][:, 0:128], 128)
+
+    def choose(h, ep, t):
+        ns = t; o = 2 + h; b = 4 + h
+        stage2(h, ns)
+        sc, sk = view("SC", h); sf, fk = view("SF", h); su, uk = view("SU", h)
+        buf = T["SC_%d" % h]; oh = T["OH_%d" % h]; ot = T["OT_%d" % h]
+        so = slot[("SC", h)]
+
+        def row(a, n): return buf[:, so[a]:so[a] + n]
+        if t == 1:
+            red([(o, "o2")], [sk("r0")], sc("r0"), B[o][:, 0:128], 128)
+            ts([(o, "o2"), sk("r0")], [("OH", h, 0)], oh[:, 0:128], B[o][:, 0:128], sc("r0"), ALU.is_equal, n=128)
+            onehot(h, 1)
+        else:
+            if t == 2:
+                ts([(b, "d")], [sk("dr1")], sc("dr1"), B[b][:, 384:385], 0.0, ALU.is_equal)
+                lin([sk("dr1")], [sk("k1")], sc("k1"), sc("dr1"), -BIG, n=1)
+                cd, ck = row("k0", 2), [sk("k0"), sk("k1")]
+            else:
+                ts([(b, "d")], [sk("e0")], sc("e0"), B[b][:, 384:385], 0.0, ALU.is_equal)
+                ts([(b, "d"), sk("cval")], [sk("e1")], sc("e1"), B[b][:, 385:386], 0.0, ALU.is_equal, sc("cval"), ALU.mult)
+                tt([sk("e0"), sk("e1")], [sk("dr2")], sc("dr2"), sc("e0"), sc("e1"), ALU.max)
+                lin([sk("dr2")], [sk("c1")], sc("c1"), sc("dr2"), -BIG, n=1)
+                cd, ck = row("c0", 3), [sk("c0"), sk("c1"), sk("c2")]
+            for s in range(ns): red([(o, "o2")], [sk("r%d" % s)], sc("r%d" % s), B[o][:, 128 * s:128 * s + 128], 128)
+            tt([sk("r%d" % s) for s in range(ns)] + ck, [sk("y")], row("y0", ns), row("r0", ns), cd, ALU.add)
+            red([sk("y")], [sk("best")], sc("best"), row("y0", ns))
+            ts(ck + [sk("best")], [sk("bias")], row("b0", ns), cd, sc("best"), ALU.subtract, 1.0, ALU.add)
+            for s in range(ns): hot([(o, "o2"), sk("bias")], [("OH", h, s)], oh[:, 128 * s:128 * s + 128], B[o][:, 128 * s:128 * s + 128], sc("b%d" % s), 128)
+            onehot(h, ns)
+            if t == 2:
+                ts([sk("y"), sk("best")], [sk("s2b")], sc("h2"), sc("y1"), sc("best"), ALU.is_equal)
+                lin([fk("DL"), sk("s2b")], [fk("xa")], sf("xa"), sf("DL"), sc("h2"))
+                tt([fk("xa"), fk("L1")], [fk("x2")], sf("x2"), sf("xa"), sf("L1"), ALU.add)
+                x = "x2"
+            else:
+                ts([sk("y"), sk("best")], [sk("s3")], row("sA", 3), row("y0", 3), sc("best"), ALU.is_equal)
+                lin([fk("L2"), sk("s3")], [fk("xa")], sf("xa"), sf("L2"), sc("sA"))
+                lin([fk("R2"), sk("s3")], [fk("xb")], sf("xb"), sf("R2"), sc("sB"))
+                lin([fk("C"), sk("s3")], [fk("xc")], sf("xc"), sf("C"), sc("sC"))
+                tt([fk("xa"), fk("xb")], [fk("xd")], sf("xd"), sf("xa"), sf("xb"), ALU.add)
+                tt([fk("xd"), fk("xc")], [fk("x3")], sf("x3"), sf("xd"), sf("xc"), ALU.add)
+                x = "x3"
+            vcopy([fk(x)], [uk("xl")], su("xl"), sf(x))
+            G = T["G_%d" % h]
+            kk = [("kt", j) for j in range(4)] + ["ktg", "ktz", uk("xl")]
+            xl = su("xl")
+            for c in range(0, NP, CP):
+                cp(kk, [("G", h, c)], G[:, c:c + CP], T.KT[:, 0:WW].indirect(xl[:, c // 16:(c + CP) // 16]), CP, CG)
+        for k in range(KN):
+            if t == 1:
+                cl = h * KN + k
+                mm([("kt", cl // 4), ("OT", h)], [(b, "kt")], B[b][:, 128 + k:256:KN], T.KT[:, 128 * cl:128 * cl + 128], ot[:, k:128:KN], n=64, cy=4.0)
+            else:
+                mm([("G", h, c) for c in range(0, NP, CP)] + [("OT", h)], [(b, "kt")], B[b][:, 128 + k:256:KN], T["G_%d" % h][:, k:NP:KN], ot[:, k:128:KN], n=64, cy=4.0)
+        if t > 1:
+            ts([fk(x)], [uk("v%d" % t)], su("v%d" % t), sf(x), float(V), ALU.min)
+            tt([fk(x), ("IV", h)], [fk("e%d" % t)], sf("e%d" % t), sf(x), T.IV[:, C * h:C * h + C], ALU.is_equal)
+        if t == 2:
+            lin([sk("s2b")], [sk("s2")], sc("nh2"), sc("h2"), -1.0, 1.0, n=1)
+            tt([fk("R1"), fk("xa")], [fk("C0")], sf("C0"), sf("R1"), sf("xa"), ALU.subtract)
+        if t == 3: tt([fk("e2"), fk("e3")], [fk("eq")], sf("eq"), sf("e2"), sf("e3"), ALU.add)
+
+    def decode(h, t):
+        b = 4 + h; xx = T["XX_%d" % h]
+        sf, fk = view("SF", h); su, uk = view("SU", h); L, R = "L%d" % t, "R%d" % t
+        tt([(b, "kt"), "MK"], [("XX", h)], xx[:], B[b][:, 128:256], T.MK[:], ALU.mult, n=128, cy=1.0)
+        mm([("XX", h), "SL"], [(b, "p")], B[b][:, 256:256 + C], xx[:], T.SL[:], n=C, cy=4.0)
+        ts([(b, "p")], [fk("y")], sf("y"), B[b][:, 256:256 + C], ZV, ALU.min, -2047.0, ALU.add)
+        ts([fk("y")], [fk("u")], sf("u"), sf("y"), MAG, ALU.add, -MAG, ALU.add)
+        if t < 3: ts([fk("u")], [uk("R")], su("R"), sf("u"), 1.0 / 4096, ALU.mult)
+        tt([fk("y"), fk("u")], [fk("t")], sf("t"), sf("y"), sf("u"), ALU.subtract)
+        if t < 3: ts([fk("t")], [uk("L")], su("L"), sf("t"), 2047.0, ALU.add)
+        lin([fk("u")], [fk(R)], sf(R), sf("u"), 1.0 / 4096)
+        lin([fk("t")], [fk(L)], sf(L), sf("t"), 1.0, 2047.0)
+
+    def count(h, n, a, b, ka, kb, m=None, km=None):
+        sf, fk = view("SF", h); sc, sk = view("SC", h)
+        f = "ne%d" % n
+        tt([ka, kb], [fk(f)], sf(f), a, b, ALU.not_equal)
+        if m is not None: tt([fk(f), km], [fk(f + "m")], sf(f + "m"), sf(f), m, ALU.mult); f = f + "m"
+        act([fk(f)], [fk("junk"), sk("D%d" % n)], sf("junk"), sf(f), accum_out=sc("D%d" % n))
+
+    def expand(h, ep, t):
+        decode(h, t)
+        sf, fk = view("SF", h); su, uk = view("SU", h); sc, sk = view("SC", h)
+        if t == 1:
+            votes(ep, h, [(su("L"), uk("L")), (su("R"), uk("R"))], NV2)
+            count(h, 0, sf("R1"), sf("L1"), fk("R1"), fk("L1"))
+            counts(h)
+            tt([fk("L1"), fk("R1")], [fk("DL")], sf("DL"), sf("R1"), sf("L1"), ALU.subtract)
+            vote_out(h, 2)
+        else:
+            ts([fk("t")], [fk("qe")], sf("qe"), sf("t"), float(Z - 2047), ALU.is_ge, float(Z), ALU.mult)
+            tt([fk("C0"), fk("qe")], [fk("C")], sf("C"), sf("C0"), sf("qe"), ALU.max)
+            vcopy([fk("C")], [uk("C")], su("C"), sf("C"))
+            votes(ep, h, [(su("L"), uk("L")), (su("R"), uk("R")), (su("C"), uk("C"))], NV3)
+            lin([sk("s2"), sk("dr1")], [sk("cinv")], sc("cinv"), sc("nh2"), sc("dr1"), n=1)
+            lin([sk("cinv")], [sk("cval")], sc("cval"), sc("cinv"), -1.0, 1.0, n=1)
+            lin([sk("s2b")], [sk("c0")], sc("c0"), sc("h2"), -16.0, 32.0, n=1)
+            lin([sk("s2b")], [sk("m0")], sc("m0"), sc("h2"), 16.0, 16.0, n=1)
+            lin([sk("cinv"), sk("m0")], [sk("c2")], sc("c2"), sc("cinv"), -BIG, sc("m0"), n=1)
+            count(h, 0, sf("R2"), sf("L2"), fk("R2"), fk("L2"))
+            count(h, 1, sf("R2"), sf("C"), fk("R2"), fk("C"))
+            counts(h)
+            vote_out(h, 3)
+
+    def coef(h, o, i, ik_, scale=1.0, sk_=None, bias=None, bk_=None):
+        sc, sk = view("SC", h)
+        R = [sk(ik_)] + ([sk(sk_)] if sk_ else []) + ([sk(bk_)] if bk_ else [])
+        lin(R, [sk(o)], sc(o), sc(i), sc(scale) if sk_ else scale, sc(bias) if bk_ else bias, n=1)
+
+    def last(h, ep):
+        decode(h, 3)
+        sf, fk = view("SF", h); sb, bk_ = view("SB", h)
+        ts([fk("t")], [bk_("live")], sb("live"), sf("t"), float(Z - 2047), ALU.is_lt)
+        for kb in range(KN // 4):
+            P = (6 if h == 0 else 0) + kb if H == 2 else [6, 7, 0, 1][kb]
+            for kl in range(4):
+                k = 4 * kb + kl
+                for mp in range(H):
+                    i = mp * KN + k
+                    mm([("LR", i), bk_("live")], [(P, "lv")], B[P][:, 128 * kl + mp:128 * kl + 128:H], T.LR[:, 128 * i:128 * i + 128], sb("live"), n=C)
+            b = (h * KN) // 4 + kb
+            cp([(P, "lv")], [("lv", b)], T.LV[:, 512 * b:512 * b + 512], B[P][:], 512)
+
+    def last2(h, ep):
+        sf, fk = view("SF", h); sb, bk_ = view("SB", h); sc, sk = view("SC", h)
+        for n, s in ((0, None), (1, "L2"), (2, "R2"), (3, "C")):
+            if s is None: count(h, n, sf("R3"), sf("L3"), fk("R3"), fk("L3"))
+            else: count(h, n, sf("R3"), sf(s), fk("R3"), fk(s), sb("live"), bk_("live"))
+        counts(h)
+        ship(h, 0, 8)
+        coef(h, "p", "sA", "s3", "nh2", "s2")
+        coef(h, "wL", "sC", "s3", "h2", "s2b", "p", "p")
+        coef(h, "wA", "p", "p", -1.0, None, "nh2", "s2")
+        coef(h, "q", "sC", "s3", "h2", "s2b")
+        coef(h, "wC", "q", "q", -1.0, None, "h2", "s2b")
+        coef(h, "p1", "sA", "s3", "h2", "s2b")
+        coef(h, "qx", "sC", "s3", "nh2", "s2")
+        coef(h, "xL", "sC", "s3", "nh2", "s2", "p1", "p1")
+        coef(h, "xA", "p1", "p1", -1.0, None, "h2", "s2b")
+        coef(h, "xC", "qx", "qx", -1.0, None, "nh2", "s2")
+        coef(h, "k1c", "dr1", "dr1", -1.0, None, 1.0)
+        coef(h, "u", "dr2", "dr2", "dr1", "dr1")
+        coef(h, "k2", "u", "u", -1.0, None, "dr1", "dr1")
+        coef(h, "t", "sB", "s3", "k2", "k2")
+        coef(h, "bL", "xL", "xL", "k1c", "k1c", "t", "t")
+        coef(h, "bA", "xA", "xA", "k1c", "k1c")
+        coef(h, "bC", "xC", "xC", "k1c", "k1c")
+        coef(h, "bB", "t", "t", -1.0, None, "k2", "k2")
+        coef(h, "v1", "dr2", "dr2", -1.0, None, 1.0)
+        coef(h, "v2", "cval", "cval")
+
+    def weigh(h, out, terms):
+        sf, fk = view("SF", h); sc, sk = view("SC", h)
+        cur = None
+        for j, (a, c) in enumerate(terms):
+            f = "%s%d" % (out, j)
+            lin([fk(a), sk(c)], [fk(f)], sf(f), sf(a), sc(c))
+            if j:
+                n = out if j == len(terms) - 1 else "%ss%d" % (out, j)
+                tt([fk(f), fk(cur)], [fk(n)], sf(n), sf(cur), sf(f), ALU.add)
+                f = n
+            cur = f
+
+    def lookups(h, ep):
+        su, uk = view("SU", h)
+        lk = [("lv", j) for j in range(4)] + [("lvz",)]
+        b = 4 + h
+        for j, (n, l) in enumerate((("GA", "v2"), ("GB", "v3"))):
+            for c in range(0, NP, CP):
+                cp(lk + [uk(l)], [(n, h, c)], T["%s_%d" % (n, h)][:, c:c + CP], T.LV[:].indirect(su(l)[:, c // 16:(c + CP) // 16]), CP, CG)
+            for i in range(16):
+                mm([("FD", i)] + [(n, h, c) for c in range(0, NP, CP)], [(b, "die")], B[b][:, 320:320 + C], T.FD[:, 128 * i:128 * i + 128], T["%s_%d" % (n, h)][:, i:NP:16], j == 0 and i == 0, j == 1 and i == 15, n=C)
+
+    def ab(h, ep):
+        sf, fk = view("SF", h); sc, sk = view("SC", h)
+        iv = T.IV[:, C * h:C * h + C]
+        weigh(h, "a", [("L3", "wL"), ("L2", "wA"), ("C", "wC")])
+        weigh(h, "b", [("L3", "bL"), ("L2", "bA"), ("C", "bC"), ("R2", "bB")])
+        o = 2 + h; p = par[h]; par[h] = 1 - p
+        dsum(h, o, p)
+        buf = T["SC_%d" % h]; so = slot[("SC", h)]
+
+        def row(a, n): return buf[:, so[a]:so[a] + n]
+        ts([(o, "d")], [sk("z")], row("z0", 4), B[o][:, 384:388], 0.0, ALU.is_equal)
+        ts([sk("z")], [sk("y")], row("y0", 3), row("z1", 3), sc("z0"), ALU.subtract)
+        tt([sk("y"), sk("s3")], [sk("q3")], row("q0", 3), row("y0", 3), row("sA", 3), ALU.mult)
+        tt([sk("z"), sk("q3")], [sk("y")], row("y0", 3), row("z1", 3), row("q0", 3), ALU.subtract)
+        tt([sk("y"), sk("v0"), sk("v1"), sk("v2")], [sk("q3")], row("q0", 3), row("y0", 3), row("v0", 3), ALU.mult)
+        red([sk("q3")], [sk("dr3")], sc("dr3"), row("q0", 3))
+        tt([fk("a"), fk("R3")], [fk("m0")], sf("m0"), sf("a"), sf("R3"), ALU.subtract)
+        lin([fk("m0"), sk("dr3")], [fk("m1")], sf("m1"), sf("m0"), sc("dr3"))
+        tt([fk("m1"), fk("R3")], [fk("m2")], sf("m2"), sf("m1"), sf("R3"), ALU.add)
+        lin([fk("m2"), sk("u")], [fk("m3")], sf("m3"), sf("m2"), sc("u"))
+        tt([fk("m3"), fk("b")], [fk("bb")], sf("bb"), sf("b"), sf("m3"), ALU.add)
+        tt([fk("a"), ("IV", h)], [fk("da")], sf("da"), sf("a"), iv, ALU.subtract)
+        tt([fk("bb"), ("IV", h)], [fk("db")], sf("db"), sf("bb"), iv, ALU.subtract)
+        lin([fk("bb")], [fk("m4")], sf("m4"), sf("bb"), 4096.0)
+        tt([fk("m4"), fk("a")], [fk("ab")], sf("ab"), sf("m4"), sf("a"), ALU.add)
+
+    def calls(h, ep):
+        sf, fk = view("SF", h); sb, bk_ = view("SB", h); su, uk = view("SU", h)
+        iv = T.IV[:, C * h:C * h + C]; b = 4 + h
+        tt([(b, "die"), fk("eq")], [fk("m1")], sf("m1"), B[b][:, 320:320 + C], sf("eq"), ALU.is_equal, cy=1.0)
+        tt([fk("m1"), bk_("live")], [fk("go")], sf("go"), sf("m1"), sb("live"), ALU.mult)
+        for n in ("a", "b"):
+            tt([fk("d" + n), fk("go")], [fk("e" + n)], sf("e" + n), sf("d" + n), sf("go"), ALU.mult)
+            tt([fk("e" + n), ("IV", h)], [fk("f" + n)], sf("f" + n), sf("e" + n), iv, ALU.add)
+            vcopy([fk("f" + n)], [uk(n)], su(n), sf("f" + n))
+
+    def pieces(h, ep):
+        sf, fk = view("SF", h); sb, bk_ = view("SB", h)
+        if ep == 1:
+            lin([fk("go")], [bk_("ng")], sb("ng"), sf("go"), -1.0, 1.0)
+            tt([fk("ab"), fk("go")], [fk("vf")], sf("vf"), sf("ab"), sf("go"), ALU.mult)
+        else:
+            lin([fk("go")], [fk("n2")], sf("n2"), sf("go"), -1.0, 1.0)
+            tt([fk("n2"), bk_("ng")], [bk_("ng")], sb("ng"), sb("ng"), sf("n2"), ALU.mult)
+            tt([fk("vf"), fk("n2")], [fk("vg")], sf("vg"), sf("vf"), sf("n2"), ALU.mult)
+            tt([fk("ab"), fk("go")], [fk("vh")], sf("vh"), sf("ab"), sf("go"), ALU.mult)
+            tt([fk("vg"), fk("vh")], [fk("vf")], sf("vf"), sf("vg"), sf("vh"), ALU.add)
+        cp([fk("vf")], [bk_("v0")], sb("v0"), sf("vf"), 64)
+        tt([fk("vf"), bk_("v0")], [fk("vr")], sf("vr"), sf("vf"), sb("v0"), ALU.subtract)
+        cp([fk("vr")], [bk_("v1")], sb("v1"), sf("vr"), 64)
+        tt([fk("vr"), bk_("v1")], [bk_("v2")], sb("v2"), sf("vr"), sb("v1"), ALU.subtract)
+
+    def neww(h, ep):
+        t = T["W%d" % ep]
+        su, uk = view("SU", h)
+        wk = [("w", ep, j) for j in range(4)] + [("wg", ep), ("wz", ep)]
+        for n, l in (("GA", "a"), ("GB", "b")):
+            for c in range(0, NP, CP):
+                cp(wk + [uk(l)], [(n, h, c)], T["%s_%d" % (n, h)][:, c:c + CP], t[:, 0:WW].indirect(su(l)[:, c // 16:(c + CP) // 16]), CP, CG)
+
+    def neww2(h, ep):
+        out = T.W2 if ep == 1 else T.W1
+        for kb in range(KN // 4):
+            P = (6 if h == 0 else 0) + kb if H == 2 else [6, 7, 0, 1][kb]
+            mm(["IB", "QT"], [(P, "nw")], B[P][:], T.IB[:], T.QT[:], True, False, n=512)
+            for n in ("GA", "GB"):
+                for kl in range(4):
+                    mm(["HB"] + [(n, h, c) for c in range(0, NP, CP)], [(P, "nw")], B[P][:, 128 * kl:128 * kl + 128], T.HB[:], T["%s_%d" % (n, h)][:, 4 * kb + kl:NP:KN], False, n == "GB" and kl == 3)
+            b = h * KN // 4 + kb
+            ts([(P, "nw")], [("w", 3 - ep, b)], out[:, 512 * b:512 * b + 512], B[P][:], 8388608.0, ALU.add, -8388608.0, ALU.add, n=512)
+            if ep == 2: dma("Y", [("w", 1, b)], [("yw", b)], T.yw[:, 512 * b:512 * b + 512], out[:, 512 * b:512 * b + 512])
+
+    def kidsout(h, ep, kb):
+        sb, bk_ = view("SB", h)
+        b = h * KN // 4 + kb
+        Pn, Pv = (6 + b % 2, b % 2) if ep == 1 else ((2, 3), (4, 5))[b % 2]
+        if ep == 1:
+            act([("w", 2, b)], [("PR", b)], T.PR[:, 512 * b:512 * b + 512], T.W2[:, 512 * b:512 * b + 512], ACT.Sign, n=512)
+            mm(["IB", "BT"], [(Pv, "vl")], B[Pv][:], T.IB[:], T.BT[:], True, False, n=512)
+            mm(["NB", ("PR", b)], [(Pv, "vl")], B[Pv][:], T.NB[:], T.PR[:, 512 * b:512 * b + 512], False, False, n=512)
+        todo = [(4 * kb + kl, kl, mp) for kl in range(4) for mp in range(H)]
+        for j, (k, kl, mp) in enumerate(todo):
+            i = mp * KN + k
+            mm([("LR", i), bk_("ng")], [(Pn, "ng")], B[Pn][:, 128 * kl + mp:128 * kl + 128:H], T.LR[:, 128 * i:128 * i + 128], sb("ng"), n=C)
+        for j, (k, kl, mp) in enumerate(todo):
+            i = mp * KN + k
+            for n in range(3):
+                mm([("LR", i), bk_("v%d" % n)], [(Pv, "vl")], B[Pv][:, 128 * kl + mp:128 * kl + 128:H], T.LR[:, 128 * i:128 * i + 128], sb("v%d" % n),
+                   ep == 2 and n == 0, n == 2 if ep == 2 else (n == 2 and j == len(todo) - 1), n=C)
+        kt = T.KT[:, 512 * b:512 * b + 512]
+        tt([("ki", b), (Pn, "ng")], [("kt", b)], kt, T.KI[:, 512 * b:512 * b + 512], B[Pn][:], ALU.mult, n=512, cy=1.0)
+        tt([("kt", b), (Pv, "vl")], [("kt", b)], kt, kt, B[Pv][:], ALU.max if ep == 1 else ALU.add, n=512, cy=1.0)
+        if ep == 2: dma("Y", [("kt", b)], [("yk", b)], T.yk[:, 512 * b:512 * b + 512], kt)
+
+    def absent(ep, b, P):
+        t = T["W%d" % ep]
+        wk = ("w", ep, b) if b < 4 else ("wg", ep)
+        mm(["IB", "BT"], [(P, "ab")], B[P][:], T.IB[:], T.BT[:], True, False, n=512)
+        mm(["NB", wk], [(P, "ab")], B[P][:], T.NB[:], t[:, 512 * b:512 * b + 512], False, True, n=512)
+        if b < 4: tt([("ki", b), (P, "ab")], [("kt", b)], T.KT[:, 512 * b:512 * b + 512], T.KI[:, 512 * b:512 * b + 512], B[P][:], ALU.max, n=512, cy=1.0)
+        else: tt(["GI", (P, "ab")], ["ktg"], T.KT[:, 512 * b:512 * b + 512], T.GI[:, 512 * b - V:512 * b - V + 512], B[P][:], ALU.max, n=512, cy=1.0)
+
+    HS = range(H)
+    for h in HS:
+        positions(1, h)
+        vote1(h)
+    for b in range(4): absent(1, b, 4 + b % 2)
+    for ep in (1, 2):
+        if ep == 2:
+            for h in HS:
+                positions(2, h)
+                vote1(h)
+            for h in HS: pieces(h, 1)
+            for h in HS:
+                for kb in range(KN // 4): kidsout(h, 1, kb)
+        for h in HS: choose(h, ep, 1)
+        for b in range(4, 7): absent(ep, b, 6 + b % 2)
+        for h in HS: expand(h, ep, 1)
+        for h in HS: choose(h, ep, 2)
+        for h in HS: expand(h, ep, 2)
+        for h in HS: choose(h, ep, 3)
+        for h in HS: last(h, ep)
+        for h in HS: last2(h, ep)
+        for h in HS: lookups(h, ep)
+        for h in HS:
+            ab(h, ep)
+            calls(h, ep)
+            neww(h, ep)
+        if ep == 1:
+            neww2(0, 1)
+            ghosts(2)
+            for h in range(1, H): neww2(h, 1)
+        else:
+            for h in HS: pieces(h, 2)
+            for h in HS:
+                for kb in range(KN // 4): kidsout(h, 2, kb)
+            for h in HS: neww2(h, 2)
+
+    n = len(nodes); pred = [set() for _ in range(n)]
+    lw = {}; lr = {}; bp = {}
+    for i, (q, R, W, _e, _c, _l) in enumerate(nodes):
+        for k in R:
+            if k in lw: pred[i].add(lw[k])
+        for k in W:
+            if k in lw: pred[i].add(lw[k])
+            pred[i].update(lr.get(k, ()))
+        for k in R + W:
+            if bk(k) is not None:
+                e = bp.setdefault(bk(k), {})
+                for q2, j in e.items():
+                    if q2 != q or q == "P": pred[i].add(j)
+        for k in R + W:
+            if bk(k) is not None: bp[bk(k)][q] = i
+        for k in R: lr.setdefault(k, []).append(i)
+        for k in W: lw[k] = i; lr[k] = []
+    succ = [[] for _ in range(n)]
+    for i in range(n):
+        pred[i].discard(i)
+        for j in pred[i]: succ[j].append(i)
+    prio = [0.0] * n
+    for i in range(n - 1, -1, -1):
+        m = max([prio[j] for j in succ[i]] or [0.0])
+        prio[i] = nodes[i][4] + nodes[i][5] + m + (WAKE if nodes[i][0] != "P" else 0.0)
+    left = [len(p) for p in pred]; est = [0.0] * n; ready = {q: [] for q in eng}; free = {q: 0.0 for q in eng}; order = []
+
+    def offer(i):
+        for q in nodes[i][0]: ready[q].append(i)
+    for i in range(n):
+        if left[i] == 0: offer(i)
+    while len(order) < n:
+        best = None
+        for q in ("S", "V", "P", "G", "Y"):
+            if ready[q]:
+                t0 = max(free[q], min(est[i] for i in ready[q]))
+                if best is None or t0 < best[0]: best = (t0, q)
+        t0, q = best
+        i = max((i for i in ready[q] if est[i] <= t0 + 1e-9), key=lambda i: (prio[i], -i))
+        for r in nodes[i][0]: ready[r].remove(i)
+        free[q] = t0 + nodes[i][4]; order.append((i, q))
+        for j in succ[i]:
+            same = nodes[j][0] == q
+            est[j] = max(est[j], free[q] + nodes[i][5] + ((0.0 if q == "P" else SELF) if same else WAKE))
+            left[j] -= 1
+            if left[j] == 0: offer(j)
+    for i, q in order: nodes[i][3](q)
+    for s in cnt:
+        g.wait_ge(T.sem[s], cnt[s])

@@ -13,38 +13,43 @@ WW = 3600
 Z = 3584
 BIG = 16777216.0
 ZV = 4097.0 * Z
+CTR = 1792
 MAG = 51539607552.0
-NV2 = (8, 4)
-NV3 = (8, 8, 4)
+NV2 = (6, 5)
+NV3 = (6, 5, 5)
+CUTS = {1: (1,), 2: (1, 2), 3: (2, 3)}
 CP = 512
 VC = 4
-CY, PE, CG, WAKE, RLAT, DLAT, SELF = 0.83e-3, 0.6e-3, 1.56, 0.06, 2.2, 2.5, 0.06
+CY, PE, CG, WAKE, RLAT, RCOL, DLAT, SELF, LEAD = 0.83e-3, 0.6e-3, 1.56, 0.08, 2.2, 0.004, 2.5, 0.06, 2.5
 
-SF = 70; SU = 8; SB = 8; SC = 96
+SF = 2; SU = 9; SB = 6; SC = 64; SH = 10
 SCRATCH = {
     "W1": ("sbuf", [128, WW], "bfloat16"), "W2": ("sbuf", [128, WW], "bfloat16"),
     "KT": ("sbuf", [128, WW], "float32"), "KI": ("sbuf", [128, V], "int32"),
     "WP": ("sbuf", [128, V], "bfloat16"), "GI": ("sbuf", [128, 3 * X], "float32"), "PR": ("sbuf", [128, V], "bfloat16"),
-    "LV": ("sbuf", [128, V + 16], "bfloat16"),
-    "LR": ("sbuf", [128, 2048], "bfloat16"), "FD": ("sbuf", [128, 2048], "bfloat16"),
+    "LV": ("sbuf", [128, WW], "bfloat16"), "KF": ("sbuf", [128, V], "float32"),
+    "LB": ("sbuf", [128, 2048], "bfloat16"), "LR": ("sbuf", [128, 2048], "bfloat16"), "FD": ("sbuf", [128, 2048], "bfloat16"),
     "IC": ("sbuf", [128, 128], "int32"), "ID": ("sbuf", [128, 128], "int32"), "IM": ("sbuf", [128, 128], "int32"), "IS": ("sbuf", [128, 64], "int32"),
-    "IV": ("sbuf", [128, 128], "float32"), "IP": ("sbuf", [128, 2], "int32"), "IQ": ("sbuf", [128, 4], "int32"), "PG": ("sbuf", [128, 8], "float32"), "CI": ("sbuf", [128, 16], "int32"), "CM": ("sbuf", [128, 16], "float32"),
-    "IB": ("sbuf", [128, 128], "bfloat16"), "NB": ("sbuf", [128, 128], "bfloat16"), "HB": ("sbuf", [128, 128], "bfloat16"), "NI": ("sbuf", [128, 128], "bfloat16"),
+    "IV": ("sbuf", [128, 128], "float16"), "IP": ("sbuf", [128, 2], "int32"), "IQ": ("sbuf", [128, 4], "int32"), "PG": ("sbuf", [128, 12], "float32"), "CI": ("sbuf", [128, 16], "int32"), "CM": ("sbuf", [128, 16], "float32"),
+    "IB": ("sbuf", [128, 128], "bfloat16"), "NB": ("sbuf", [128, 128], "bfloat16"), "HB": ("sbuf", [128, 128], "bfloat16"), "NI": ("sbuf", [128, 128], "bfloat16"), "I4": ("sbuf", [128, 128], "bfloat16"),
+    "A0": ("sbuf", [128, 128], "bfloat16"), "AN": ("sbuf", [128, 128], "bfloat16"), "AS": ("sbuf", [128, 128], "bfloat16"), "NT": ("sbuf", [128, 128], "bfloat16"),
+    "ON": ("sbuf", [128, 512], "bfloat16"), "DC": ("sbuf", [128, 384], "bfloat16"),
     "BT": ("sbuf", [128, 512], "bfloat16"), "QT": ("sbuf", [128, 512], "bfloat16"),
     "CB": ("sbuf", [128, 384], "bfloat16"), "F": ("sbuf", [128, 128], "float16"), "E": ("sbuf", [128, 128], "float16"),
-    "GQ": ("sbuf", [128, 128], "bfloat16"), "MK": ("sbuf", [128, 128], "bfloat16"), "SL": ("sbuf", [128, C], "float32"),
-    "T1": ("sbuf", [128, 128], "float32"), "T2": ("sbuf", [128, 128], "float32"), "T3": ("sbuf", [128, 128], "float32"),
+    "GQ": ("sbuf", [128, 128], "bfloat16"), "MK": ("sbuf", [128, 128], "float32"), "SL": ("sbuf", [128, C], "float32"),
+    "T1": ("sbuf", [128, 128], "float32"), "T2": ("sbuf", [128, 384], "float32"), "T3": ("sbuf", [128, 128], "float32"),
 }
 for _j in range(7): SCRATCH["IT%d" % _j] = ("sbuf", [128, 128], "int32")
 for _h in range(H):
     for _n, _w, _t in (("G", NP, "float32"), ("M0", NP, "bfloat16"), ("M1", NP, "bfloat16"), ("M2", NP, "bfloat16"), ("RW", NP, "bfloat16"),
                        ("GA", NP, "bfloat16"), ("GB", NP, "bfloat16"), ("SND0", 392, "float16"), ("SND1", 392, "float16"), ("LND0", 3 * 392, "float16"),
                        ("LND1", 3 * 392, "float16"), ("OH", 384, "bfloat16"), ("OT", 128, "float32"), ("XX", 128, "float32"),
-                       ("SF", SF * C, "float32"), ("SU", SU * C, "uint16"), ("SB", SB * C, "bfloat16"), ("SC", SC, "float32")):
+                       ("SF", SF * C, "float32"), ("SU", SU * C, "uint16"), ("SB", SB * C, "bfloat16"), ("SH", SH * C, "float16"), ("DG", 12 * 128, "bfloat16"),
+                       ("JK", 16, "float32"), ("SC", SC, "float32")):
         SCRATCH["%s_%d" % (_n, _h)] = ("sbuf", [128, _w], _t)
 for _b in range(8):
     SCRATCH["B%d" % _b] = ("psum", [128, 512], "float32")
-SEMAPHORES = ["cV", "cS", "cP", "cG"] + ["d%d" % i for i in range(44)] + ["a%d" % i for i in range(22)] + ["l%d" % i for i in range(22)]
+SEMAPHORES = ["cV", "cS", "cP", "cG"] + ["d%d" % i for i in range(44)] + ["a%d" % i for i in range(34)] + ["l%d" % i for i in range(34)]
 
 
 def rank_program(g, core, T, topo):
@@ -52,7 +57,7 @@ def rank_program(g, core, T, topo):
     if rank is None:
         return
     eng = {"V": g.vector, "S": g.scalar, "P": g.tensor, "G": g, "Y": g.sync}
-    cnt = {}; known = {q: {} for q in eng}; wr = {}; rd = {}; bank = {}; snap = {}; nd = [0, 0]
+    cnt = {}; known = {q: {} for q in eng}; wr = {}; rd = {}; bank = {}; snap = {}; nd = [0, 0]; half = [None]
     nodes = []
 
     def put(d, k, s, v):
@@ -94,7 +99,7 @@ def rank_program(g, core, T, topo):
         mark(R, W, s, cnt[s])
 
     def node(q, R, W, emit, cost, lat=0.0):
-        nodes.append([q, list(R), list(W), emit, cost, lat])
+        nodes.append([q, list(R), list(W), emit, cost, lat, half[0]])
 
     def op(q, R, W, make, n=64, cy=1.0):
         cost = 0.06 + max(64, n * cy) * CY if q != "P" else cy * max(64, n) * PE
@@ -130,7 +135,7 @@ def rank_program(g, core, T, topo):
             cnt[a] = 3 * n; cnt[l] = n
             mark(R, (), l, n); snap[(l, n)] = dict(known["G"])
             for k in W: wr[k] = {a: 3 * n}
-        node("G", R, W, emit, 0.6, RLAT)
+        node("G", R, W, emit, 0.6, RLAT + RCOL * src.shape[1])
 
     def ts(R, W, o, i, s1, op0, s2=None, op1=None, n=64, cy=1.0):
         if op1 is None: op("V", R, W, lambda e, q: e.tensor_scalar(o, i, s1, None, op0), n, cy)
@@ -138,6 +143,7 @@ def rank_program(g, core, T, topo):
 
     def tt(R, W, o, a, b, f, n=64, cy=2.0): op("V", R, W, lambda e, q: e.tensor_tensor(o, a, b, f), n, cy)
     def red(R, W, o, i, n=64): op("V", R, W, lambda e, q: e.tensor_reduce(o, i, AxisListType.X, ALU.max), n)
+    def redn(R, W, o, i, n=64): op("V", R, W, lambda e, q: e.tensor_reduce(o, i, AxisListType.X, ALU.max, negate=True), n)
     def vcopy(R, W, o, i, n=64): op("V", R, W, lambda e, q: e.tensor_copy(o, i), n)
     def fill(W, o, c, n=64): op("V", (), W, lambda e, q: e.memset(o, c), n)
     def mm(R, W, o, l, r, st=True, sp=True, n=128, cy=1.0): op("P", R, W, lambda e, q: e.matmul(o, l, r, st, sp), n, cy)
@@ -169,9 +175,9 @@ def rank_program(g, core, T, topo):
         return (lambda n: arr(kind, h, n)), (lambda n: (kind, h, n))
 
     for b in range(4):
-        dma("Y", (), [("w", 1, b)], T.W1[:, 512 * b:512 * b + 512], T.w[:, 512 * b:512 * b + 512])
+        dma("YS"[b % 2], (), [("w", 1, b)], T.W1[:, 512 * b:512 * b + 512], T.w[:, 512 * b:512 * b + 512])
     for b in range(4):
-        dma("S", (), [("ki", b)], T.KI[:, 512 * b:512 * b + 512], T.kids[:, 512 * b:512 * b + 512])
+        dma("Y", (), [("ki", b)], T.KI[:, 512 * b:512 * b + 512], T.kids[:, 512 * b:512 * b + 512])
     iota(["IC"], T.IC[:], [[1, 128]], 0, 0, 128)
     iota(["ID"], T.ID[:], [[1, 128]], 128, -1, 128)
     iota(["IP"], T.IP[:, 0:2], [[0, 2]], 0, 1, 32)
@@ -189,6 +195,7 @@ def rank_program(g, core, T, topo):
     IT = [T["IT%d" % j] for j in range(7)]
     ts(["ID"], ["IB"], T.IB[:], T.ID[:], 128.0, ALU.is_equal, n=128)
     fill(["BT"], T.BT[:], BIG, n=256)
+    fill(["ON"], T.ON[:], 1.0, n=256)
     lin(["IB"], ["NB"], T.NB[:], T.IB[:], -BIG, n=128)
     ts(["ID"], ["IT0"], IT[0][:], T.ID[:], KN - 1, ALU.bitwise_and, n=128)
     ts(["IT0"], ["F"], T.F[:], IT[0][:], 0.0, ALU.is_equal, 64.0, ALU.mult, n=128)
@@ -199,16 +206,27 @@ def rank_program(g, core, T, topo):
     ts(["IT1", "PG"], ["GQ"], T.GQ[:], IT[1][:], T.PG[:, 0:1], ALU.is_equal, n=128)
     lin(["GQ"], ["T1"], T.T1[:], T.GQ[:], BIG, -BIG, n=128)
     ts(["IC"], ["IT2"], IT[2][:], T.IC[:], 15, ALU.bitwise_and, n=128)
-    ts(["IT2"], ["T2"], T.T2[:], IT[2][:], -1.0, ALU.mult, 15.0, ALU.add, n=128)
-    for s in range(3): tt(["T1", "T2"], [("CB", s)], T.CB[:, 128 * s:128 * s + 128], T.T1[:], T.T2[:], ALU.add, n=128)
+    for s in range(3):
+        ts(["IT2"], [("T2", s)], T.T2[:, 128 * s:128 * s + 128], IT[2][:], -1.0, ALU.mult, 15.0 + (32.0, 0.0, 16.0)[s], ALU.add, n=128)
+        tt(["T1", ("T2", s)], [("CB", s)], T.CB[:, 128 * s:128 * s + 128], T.T1[:], T.T2[:, 128 * s:128 * s + 128], ALU.add, n=128)
     CBK = [("CB", 0), ("CB", 1), ("CB", 2)]
+    for s in range(3): fill([("DC", s)], T.DC[:, 128 * s:128 * s + 128], (-16.0, 0.0, 16.0)[s], n=64)
+    DCK = [("DC", s) for s in range(3)]
+    fill(["NT"], T.NT[:], -BIG, n=64)
     ts(["IM"], ["IT3"], IT[3][:], T.IM[:], LK, ALU.arith_shift_right, H - 1, ALU.bitwise_and, n=128)
-    ts(["IT3"], ["MK"], T.MK[:], IT[3][:], 0.0, ALU.is_equal, n=128)
+    ts(["IT3"], ["MK"], T.MK[:], IT[3][:], 0.0, ALU.is_equal, ZV, ALU.mult, n=128)
     ts(["IS"], ["IT4"], IT[4][:, 0:C], T.IS[:, 0:C], LH, ALU.arith_shift_right)
     ts(["IT4"], ["SL"], T.SL[:], IT[4][:, 0:C], 0.0, ALU.is_equal)
     lin(["IB"], ["NI"], T.NI[:], T.IB[:], -1.0, n=128)
+    lin(["IB"], ["I4"], T.I4[:], T.IB[:], 4.0, n=128)
     ts(["F"], ["T3"], T.T3[:], T.F[:], 1.0 / 64, ALU.mult, n=128)
     tt(["T3", "GQ"], ["E"], T.E[:], T.T3[:], T.GQ[:], ALU.mult, n=128)
+    for j in range(3): ts(["IP"], [("PC", j)], T.PG[:, 4 + j:5 + j], T.IP[:, 0:1], float(j), ALU.is_equal, (4096.0 * CTR, float(CTR), BIG)[j], ALU.mult)
+    tt([("PC", 0), ("PC", 1)], ["P1"], T.PG[:, 7:8], T.PG[:, 4:5], T.PG[:, 5:6], ALU.add)
+    tt(["P1", ("PC", 2)], ["P2"], T.PG[:, 8:9], T.PG[:, 7:8], T.PG[:, 6:7], ALU.add)
+    ts(["ON", "P1"], ["A0"], T.A0[:], T.ON[:, 0:128], T.PG[:, 7:8], ALU.mult)
+    ts(["ON", "P1"], ["AN"], T.AN[:], T.ON[:, 0:128], T.PG[:, 7:8], ALU.mult, -1.0, ALU.mult)
+    ts(["ON", "P2"], ["AS"], T.AS[:], T.ON[:, 0:128], T.PG[:, 8:9], ALU.mult)
     for ep in (1, 2): fill([("wz", ep)], T["W%d" % ep][:, Z:WW], 0.0)
     fill(["ktz"], T.KT[:, Z:WW], BIG)
     ts(["IQ1"], ["IQ2"], T.IQ[:, 2:3], T.IQ[:, 1:2], KN - 1, ALU.bitwise_and)
@@ -216,49 +234,46 @@ def rank_program(g, core, T, topo):
     ts(["IQ2"], ["PG2"], T.PG[:, 2:3], T.IQ[:, 2:3], 128.0, ALU.mult)
     tt(["PG2", "IQ3"], ["PG3"], T.PG[:, 3:4], T.PG[:, 2:3], T.IQ[:, 3:4], ALU.add)
     for h in range(H):
-        ts(["IC"], [("IT", 5 + h)], IT[5 + h][:, 0:C], T.IC[:, 0:C], float(H), ALU.mult, float(h * KN * 128), ALU.add)
+        ts(["IC"], [("IT", 5 + h)], IT[5 + h][:, 0:C], T.IC[:, 0:C], float(H), ALU.mult, float(h * KN * 128 - CTR), ALU.add)
         ts([("IT", 5 + h), "PG3"], [("IV", h)], T.IV[:, C * h:C * h + C], IT[5 + h][:, 0:C], T.PG[:, 3:4], ALU.add)
     ts(["CI", "PG"], ["CM"], T.CM[:], T.CI[:], T.PG[:, 1:2], ALU.is_equal)
-    fill([("lvz",)], T.LV[:, V:V + 16], 0.0)
+    fill([("lvz",)], T.LV[:, V:WW], 0.0, n=(WW - V) // 2)
     fill(["QT"], T.QT[:], -0.25, n=256)
     lin(["IB"], ["HB"], T.HB[:], T.IB[:], 0.5, n=128)
     for h in range(H):
         sc, sk = view("SC", h)
         slot[("SC", h)] = {("D%d" % n): n for n in range(8)}
-        for n in ("k0", "k1", "r0", "r1", "r2", "c0", "c1", "c2", "sA", "sB", "sC", "z0", "z1", "z2", "z3", "v0", "v1", "v2", "y0", "y1", "y2", "b0", "b1", "b2", "q0", "q1", "q2"): sc(n)
+        for n in ["%s%d" % (a, j) for a, m in (("r", 3), ("s", 6), ("f", 6), ("p", 6), ("n", 6)) for j in range(m)]: sc(n)
+        slot[("SH", h)] = {n: j for j, n in enumerate(("L1", "R1", "L2", "R2", "L3", "R3", "C", "ma", "mb", "nv"))}
+        slot[("SU", h)] = {n: j for j, n in enumerate(("L1", "R1", "L2", "R2", "C", "x2", "x3", "a", "b"))}
         fill([sk("D%d" % n) for n in range(8)], T["SC_%d" % h][:, 0:8], 0.0)
-        fill([sk("k0")], sc("k0"), 16.0)
-        fill([sk("v0")], sc("v0"), 1.0)
+        fill([sk("f1")], sc("f1"), 0.0)
     for i in range(16):
         act(["GQ", "CM"], [("LR", i)], T.LR[:, 128 * i:128 * i + 128], T.GQ[:], scale=T.CM[:, i:i + 1], n=128)
     for i in range(16):
         act(["IB", "CM"], [("FD", i)], T.FD[:, 128 * i:128 * i + 128], T.IB[:], scale=T.CM[:, i:i + 1], n=128)
 
-    def positions(ep, h):
-        t = T["W%d" % ep]
+    def row(h, a, n):
+        j = slot[("SC", h)][a]
+        return T["SC_%d" % h][:, j:j + n]
+
+    def positions(h):
         for b in range(NP // 512):
-            P = (2 if h else 6) + b if H == 2 else 4 + b
+            P = (2 if h else 6) + b
             n = 512 // KN
             for k in range(KN):
                 cl = (h * KN + k)
-                mm(["IB", ("w", ep, cl // 4)], [(P, "wp")], B[P][:, k:512:KN], T.IB[:], t[:, 128 * cl + n * b:128 * cl + n * b + n], n=n)
+                mm(["IB", ("w", 1, cl // 4)], [(P, "wp")], B[P][:, k:512:KN], T.IB[:], T.W1[:, 128 * cl + n * b:128 * cl + n * b + n], n=n)
             cp([(P, "wp")], [("WP", h, b)], T.WP[:, h * NP + 512 * b:h * NP + 512 * b + 512], B[P][:], 512)
 
     par = [0] * H
 
-    def ship(h, lo, hi):
-        p = par[h]
-        ln = T["LND%d_%d" % (p, h)]
-        send(([("SD", h, p)] if lo == 0 else []) + ([("SV", h, p)] if hi > 8 else []), [("LD", h, p)], T["SND%d_%d" % (p, h)][:, lo:hi], [ln[:, 392 * d + lo:392 * d + hi] for d in range(3)])
-
-    def counts(h):
-        p = par[h]
-        vcopy([("SC", h, "D%d" % n) for n in range(8)], [("SD", h, p)], T["SND%d_%d" % (p, h)][:, 0:8], T["SC_%d" % h][:, 0:8])
-
-    def vote_out(h, ns):
-        p = par[h]
-        vcopy([(h, "o1")], [("SV", h, p)], T["SND%d_%d" % (p, h)][:, 8:8 + 128 * ns], B[h][:, 0:128 * ns], n=128 * ns)
-        ship(h, 0 if ns > 1 else 8, 8 + 128 * ns)
+    def ship(h, a, b, head):
+        p = par[h]; sn = T["SND%d_%d" % (p, h)]; ln = T["LND%d_%d" % (p, h)]
+        lo, hi = (0 if head else 8 + 128 * a), 8 + 128 * b
+        vcopy([(h, "o1")], [("SV", h, p, a)], sn[:, 8 + 128 * a:hi], B[h][:, 128 * a:128 * b], n=128 * (b - a))
+        R = [("SV", h, p, a)] + ([("SD", h, p)] if head else []) + ([("SC", h, "dr1")] if b == 3 else [])
+        send(R, [("LD", h, p, s) for s in range(a, b)] + ([("LD", h, p, "d")] if head else []), sn[:, lo:hi], [ln[:, 392 * d + lo:392 * d + hi] for d in range(3)])
 
     def stage1(h, s, src, key, c, st, sp, rhs="IB"):
         mm([rhs] + key, [(h, "o1")], B[h][:, 128 * s:128 * s + 128], src[:, 128 * c:128 * c + 128], T[rhs][:], st, sp)
@@ -266,22 +281,22 @@ def rank_program(g, core, T, topo):
     def vote1(h):
         w = T.WP[:, h * NP:h * NP + NP]
         for c in range(NC): stage1(h, 0, w, [("WP", h, c // 4)], c, c == 0, c == NC - 1)
-        vote_out(h, 1)
+        ship(h, 0, 1, False)
 
     def vgather(R, W, m, win, l, w, n): op("V", R, W, lambda e, q: e.tensor_tensor(m, win.indirect(l), w, ALU.min), n, CG)
 
-    def votes(ep, h, lists, nv):
-        win = T["W%d" % ep][:, 0:WW]
+    def votes(ep, h, lists, nv, apart):
+        win = T["W%d" % ep][:, 0:WW]; p = par[h]
         wk = [("w", ep, b) for b in range(4)] + [("wg", ep), ("wz", ep)]
         wp = T.WP[:, h * NP:h * NP + NP]
         for s, (l, lk) in enumerate(lists):
             n = nv[s]; m = T["M%d_%d" % (s, h)]; rw = T["RW_%d" % h]
             for c in range(n, NC, 4):
-                e = min(c + 4, NC); k = 128 * (e - c)
-                act(wk + [lk], [("RW", h, c)], rw[:, 128 * c:128 * e], win.indirect(l[:, 8 * c:8 * e]), n=k, cy=CG)
+                e = min(c + 4, NC); k = 128 * (e - c); rk = [("RW", h, j) for j in range(c, e)]
+                act(wk + [lk], rk, rw[:, 128 * c:128 * e], win.indirect(l[:, 8 * c:8 * e]), n=k, cy=CG)
                 P = 6 + h
                 mm(["IB"] + [("WP", h, j) for j in sorted({c // 4, (e - 1) // 4})], [(P, "df")], B[P][:, 0:k], T.IB[:], wp[:, 128 * c:128 * e], True, False, n=k)
-                mm(["NI", ("RW", h, c)], [(P, "df")], B[P][:, 0:k], T.NI[:], rw[:, 128 * c:128 * e], False, True, n=k)
+                mm(["NI"] + rk, [(P, "df")], B[P][:, 0:k], T.NI[:], rw[:, 128 * c:128 * e], False, True, n=k)
                 act([(P, "df")], [("M", h, s, j) for j in range(c, e)], m[:, 128 * c:128 * e], B[P][:, 0:k], ACT.Relu, n=k)
             for c in range(0, n, VC):
                 e = min(c + VC, n)
@@ -290,143 +305,148 @@ def rank_program(g, core, T, topo):
             todo = [(wp, [("WP", h, c // 4)], c, "IB") for c in range(n, NC)] + [(m, [("M", h, s, c)], c, "IB") for c in range(n)] \
                 + [(m, [("M", h, s, c)], c, "NI") for c in range(n, NC)]
             for j, (src, key, c, r) in enumerate(todo): stage1(h, s, src, key, c, j == 0, j == len(todo) - 1, r)
+            cuts = CUTS[len(lists)]
+            if s + 1 in cuts:
+                a = max([0] + [k for k in cuts if k <= s])
+                if a == 0: distance(h, *apart)
+                ship(h, a, s + 1, a == 0)
 
-    def dsum(h, o, p):
-        ln = T["LND%d_%d" % (p, h)]
+    def distance(h, a, b):
+        sh, hk = view("SH", h); sf, fk = view("SF", h); sc, sk = view("SC", h); o = 4 + h; p = par[h]
+        df = B[o][:, 448:512]
+        mm(["IB", hk(a)], [(o, "ne")], df, T.IB[:], sh(a), True, False, n=C)
+        mm(["NI", hk(b)], [(o, "ne")], df, T.NI[:], sh(b), False, True, n=C)
+        act([(o, "ne")], [fk("junk"), sk("D0")], sf("junk"), df, ACT.Abs, scale=1.0 / 64, accum_out=sc("D0"))
+        vcopy([sk("D%d" % n) for n in range(8)], [("SD", h, p)], T["SND%d_%d" % (p, h)][:, 0:8], T["SC_%d" % h][:, 0:8])
+
+    def dsum(h, p):
+        ln = T["LND%d_%d" % (p, h)]; o = 4 + h
         mm(["E", ("SD", h, p)], [(o, "d")], B[o][:, 384:392], T.E[:], T["SND%d_%d" % (p, h)][:, 0:8], True, False, n=8)
-        for d in range(3): mm(["E", ("LD", h, p)], [(o, "d")], B[o][:, 384:392], T.E[:], ln[:, 392 * d:392 * d + 8], False, d == 2, n=8)
+        for d in range(3): mm(["E", ("LD", h, p, "d")], [(o, "d")], B[o][:, 384:392], T.E[:], ln[:, 392 * d:392 * d + 8], False, d == 2, n=8)
 
     def stage2(h, ns):
         p = par[h]; par[h] = 1 - p
         ln = T["LND%d_%d" % (p, h)]; sn = T["SND%d_%d" % (p, h)]
         o = 2 + h; w = 128 * ns
-        if ns > 1: dsum(h, 4 + h, p)
         mm(CBK + ["IB"], [(o, "o2")], B[o][:, 0:w], T.IB[:], T.CB[:, 0:w], True, False, n=w)
-        mm(["F", ("SV", h, p)], [(o, "o2")], B[o][:, 0:w], T.F[:], sn[:, 8:8 + w], False, False, n=w)
-        for d in range(3): mm(["F", ("LD", h, p)], [(o, "o2")], B[o][:, 0:w], T.F[:], ln[:, 392 * d + 8:392 * d + 8 + w], False, d == 2, n=w)
+        if ns == 3:
+            mm(DCK + [("DG", h, "q1")], [(o, "o2")], B[o][:, 0:w], T["DG_%d" % h][:, 128:256], T.DC[:], False, False, n=w)
+            mm(["NT", ("DG", h, "dr")], [(o, "o2")], B[o][:, 256:384], T["DG_%d" % h][:, 256:384], T.NT[:], False, False, n=128)
+        for a, e in zip((0,) + CUTS[ns], CUTS[ns]):
+            x, y = 128 * a, 128 * e
+            mm(["F", ("SV", h, p, a)], [(o, "o2")], B[o][:, x:y], T.F[:], sn[:, 8 + x:8 + y], False, False, n=y - x)
+            for d in range(3):
+                mm(["F"] + [("LD", h, p, s) for s in range(a, e)], [(o, "o2")], B[o][:, x:y], T.F[:], ln[:, 392 * d + 8 + x:392 * d + 8 + y], False, d == 2 and e == ns, n=y - x)
+        return p
 
     def onehot(h, ns):
         oh = T["OH_%d" % h]; b = 4 + h
-        for s in range(ns): mm([("OH", h, s), "IB"], [(b, "ot")], B[b][:, 0:128], oh[:, 128 * s:128 * s + 128], T.IB[:], s == 0, s == ns - 1)
+        for s in range(ns): mm([("OH", h), "IB"], [(b, "ot")], B[b][:, 0:128], oh[:, 128 * s:128 * s + 128], T.IB[:], s == 0, s == ns - 1)
         cp([(b, "ot")], [("OT", h)], T["OT_%d" % h][:], B[b][:, 0:128], 128)
+
+    def diag(h, name, j, col, ck):
+        d = T["DG_%d" % h][:, 128 * j:128 * j + 128]
+        op("VS", ["IB"] + ck, [("DG", h, name)], lambda e, q: e.tensor_scalar(d, T.IB[:], col, None, ALU.mult) if q == "V" else e.activation(d, T.IB[:], ACT.Copy, scale=col), 96)
+        return d
 
     def choose(h, ep, t):
         ns = t; o = 2 + h; b = 4 + h
-        stage2(h, ns)
-        sc, sk = view("SC", h); sf, fk = view("SF", h); su, uk = view("SU", h)
-        buf = T["SC_%d" % h]; oh = T["OH_%d" % h]; ot = T["OT_%d" % h]
-        so = slot[("SC", h)]
-
-        def row(a, n): return buf[:, so[a]:so[a] + n]
+        p = stage2(h, ns)
+        sc, sk = view("SC", h); su, uk = view("SU", h); sh, hk = view("SH", h); sb, bk_ = view("SB", h)
+        oh = T["OH_%d" % h]; ot = T["OT_%d" % h]
+        x = B[o][:, 384:448]
         if t == 1:
             red([(o, "o2")], [sk("r0")], sc("r0"), B[o][:, 0:128], 128)
-            ts([(o, "o2"), sk("r0")], [("OH", h, 0)], oh[:, 0:128], B[o][:, 0:128], sc("r0"), ALU.is_equal, n=128)
+            ts([(o, "o2"), sk("r0")], [("OH", h)], oh[:, 0:128], B[o][:, 0:128], sc("r0"), ALU.is_equal, n=128)
             onehot(h, 1)
         else:
+            for s in range(ns): redn([(o, "o2")], [sk("r%d" % s)], sc("r%d" % s), B[o][:, 128 * s:128 * s + 128], 128)
             if t == 2:
-                ts([(b, "d")], [sk("dr1")], sc("dr1"), B[b][:, 384:385], 0.0, ALU.is_equal)
-                lin([sk("dr1")], [sk("k1")], sc("k1"), sc("dr1"), -BIG, n=1)
-                cd, ck = row("k0", 2), [sk("k0"), sk("k1")]
+                ts([sk("r0"), sk("r1")], [sk("bias")], sc("bias"), sc("r1"), sc("r0"), ALU.min, 1.0, ALU.add)
+                ts([sk("r0"), sk("r1")], [sk("f2")], sc("f2"), sc("r1"), sc("r0"), ALU.is_lt)
+                ts([sk("r0"), sk("r1")], [sk("f0")], sc("f0"), sc("r1"), sc("r0"), ALU.is_gt)
+                lists = [("f0", "q0", 0, "L1"), ("f2", "q1", 1, "R1")]
             else:
-                ts([(b, "d")], [sk("e0")], sc("e0"), B[b][:, 384:385], 0.0, ALU.is_equal)
-                ts([(b, "d"), sk("cval")], [sk("e1")], sc("e1"), B[b][:, 385:386], 0.0, ALU.is_equal, sc("cval"), ALU.mult)
-                tt([sk("e0"), sk("e1")], [sk("dr2")], sc("dr2"), sc("e0"), sc("e1"), ALU.max)
-                lin([sk("dr2")], [sk("c1")], sc("c1"), sc("dr2"), -BIG, n=1)
-                cd, ck = row("c0", 3), [sk("c0"), sk("c1"), sk("c2")]
-            for s in range(ns): red([(o, "o2")], [sk("r%d" % s)], sc("r%d" % s), B[o][:, 128 * s:128 * s + 128], 128)
-            tt([sk("r%d" % s) for s in range(ns)] + ck, [sk("y")], row("y0", ns), row("r0", ns), cd, ALU.add)
-            red([sk("y")], [sk("best")], sc("best"), row("y0", ns))
-            ts(ck + [sk("best")], [sk("bias")], row("b0", ns), cd, sc("best"), ALU.subtract, 1.0, ALU.add)
-            for s in range(ns): hot([(o, "o2"), sk("bias")], [("OH", h, s)], oh[:, 128 * s:128 * s + 128], B[o][:, 128 * s:128 * s + 128], sc("b%d" % s), 128)
+                ts([sk("r0"), sk("r1")], [sk("m")], sc("m"), sc("r1"), sc("r0"), ALU.min)
+                ts([sk("m"), sk("r2")], [sk("bias")], sc("bias"), sc("r2"), sc("m"), ALU.min, 1.0, ALU.add)
+                ts([sk("bias")] + [sk("r%d" % s) for s in range(3)], [sk("s%d" % s) for s in range(3)], row(h, "s0", 3), row(h, "r0", 3), sc("bias"), ALU.subtract, -1.0, ALU.is_equal)
+                lists = [("s0", "q0", 0, "L2"), ("s1", "q1", 1, "R2"), ("s2", "q2", 3, "C")]
+            hot([(o, "o2"), sk("bias")], [("OH", h)], oh[:, 0:128 * ns], B[o][:, 0:128 * ns], sc("bias"), 128 * ns)
             onehot(h, ns)
-            if t == 2:
-                ts([sk("y"), sk("best")], [sk("s2b")], sc("h2"), sc("y1"), sc("best"), ALU.is_equal)
-                lin([fk("DL"), sk("s2b")], [fk("xa")], sf("xa"), sf("DL"), sc("h2"))
-                tt([fk("xa"), fk("L1")], [fk("x2")], sf("x2"), sf("xa"), sf("L1"), ALU.add)
-                x = "x2"
-            else:
-                ts([sk("y"), sk("best")], [sk("s3")], row("sA", 3), row("y0", 3), sc("best"), ALU.is_equal)
-                lin([fk("L2"), sk("s3")], [fk("xa")], sf("xa"), sf("L2"), sc("sA"))
-                lin([fk("R2"), sk("s3")], [fk("xb")], sf("xb"), sf("R2"), sc("sB"))
-                lin([fk("C"), sk("s3")], [fk("xc")], sf("xc"), sf("C"), sc("sC"))
-                tt([fk("xa"), fk("xb")], [fk("xd")], sf("xd"), sf("xa"), sf("xb"), ALU.add)
-                tt([fk("xd"), fk("xc")], [fk("x3")], sf("x3"), sf("xd"), sf("xc"), ALU.add)
-                x = "x3"
-            vcopy([fk(x)], [uk("xl")], su("xl"), sf(x))
+            ds = [diag(h, q, j, sc(f), [sk(f)]) for f, q, j, l in lists]
+            for i, (f, q, j, l) in enumerate(lists):
+                mm([("DG", h, q), hk(l)], [(o, "xc")], x, ds[i], sh(l), i == 0, i == ns - 1, n=C)
+            xn = "x%d" % t
+            ts([(o, "xc")], [uk(xn)], su(xn), x, float(CTR), ALU.add)
             G = T["G_%d" % h]
-            kk = [("kt", j) for j in range(4)] + ["ktg", "ktz", uk("xl")]
-            xl = su("xl")
+            kk = [("kt", j) for j in range(4)] + [("ktg", j) for j in (4, 5, 6)] + ["ktz", uk(xn)]
+            xl = su(xn)
             for c in range(0, NP, CP):
                 cp(kk, [("G", h, c)], G[:, c:c + CP], T.KT[:, 0:WW].indirect(xl[:, c // 16:(c + CP) // 16]), CP, CG)
+            tt([(o, "xc"), ("IV", h)], [bk_("e%d" % t)], sb("e%d" % t), x, T.IV[:, C * h:C * h + C], ALU.is_equal, cy=1.0)
         for k in range(KN):
             if t == 1:
                 cl = h * KN + k
                 mm([("kt", cl // 4), ("OT", h)], [(b, "kt")], B[b][:, 128 + k:256:KN], T.KT[:, 128 * cl:128 * cl + 128], ot[:, k:128:KN], n=64, cy=4.0)
             else:
                 mm([("G", h, c) for c in range(0, NP, CP)] + [("OT", h)], [(b, "kt")], B[b][:, 128 + k:256:KN], T["G_%d" % h][:, k:NP:KN], ot[:, k:128:KN], n=64, cy=4.0)
-        if t > 1:
-            ts([fk(x)], [uk("v%d" % t)], su("v%d" % t), sf(x), float(V), ALU.min)
-            tt([fk(x), ("IV", h)], [fk("e%d" % t)], sf("e%d" % t), sf(x), T.IV[:, C * h:C * h + C], ALU.is_equal)
+        return p
+
+    def drops(h, t, p):
+        sc, sk = view("SC", h); b = 4 + h
+        dsum(h, p)
         if t == 2:
-            lin([sk("s2b")], [sk("s2")], sc("nh2"), sc("h2"), -1.0, 1.0, n=1)
-            tt([fk("R1"), fk("xa")], [fk("C0")], sf("C0"), sf("R1"), sf("xa"), ALU.subtract)
-        if t == 3: tt([fk("e2"), fk("e3")], [fk("eq")], sf("eq"), sf("e2"), sf("e3"), ALU.add)
+            ts([(b, "d")], [sk("dr1")], sc("dr1"), B[b][:, 384:385], 0.0, ALU.is_equal)
+            diag(h, "dr", 2, sc("dr1"), [sk("dr1")])
+            cp([sk("f2")], [sk("f3")], sc("f3"), sc("f2"), 1)
+            lin([sk("dr1"), sk("f0")], [sk("f5")], sc("f5"), sc("dr1"), -1.0, sc("f0"), n=1)
+        else:
+            ts([(b, "d"), sk("dr1")], [sk("bR")], sc("bR"), B[b][:, 384:385], 0.0, ALU.is_equal, sc("dr1"), ALU.mult)
+            lin([sk("bR"), sk("dr1")], [sk("f4")], sc("f4"), sc("bR"), -1.0, sc("dr1"), n=1)
+            cp([sk("s%d" % j) for j in range(3)], [sk("s%d" % j) for j in range(3, 6)], row(h, "s3", 3), row(h, "s0", 3), 3)
+            F6 = [sk("f%d" % j) for j in range(6)]; P6 = [sk("p%d" % j) for j in range(6)]; N6 = [sk("n%d" % j) for j in range(6)]
+            tt(F6 + [sk("s%d" % j) for j in range(6)], P6, row(h, "p0", 6), row(h, "s0", 6), row(h, "f0", 6), ALU.mult, n=6)
+            tt(F6 + P6, N6, row(h, "n0", 6), row(h, "f0", 6), row(h, "p0", 6), ALU.subtract, n=6)
+            for j, n in ((0, "wL"), (3, "bL")):
+                act(P6[j:j + 3], [sk("junk%d" % j), sk(n)], T["JK_%d" % h][:, 4 * j:4 * j + 3], row(h, "p%d" % j, 3), accum_out=sc(n), n=3)
+            for j, n in enumerate(("n0", "n2", "wL", "n3", "n5", "n4", "bL", "bR")): diag(h, "c" + n, 4 + j, sc(n), [sk(n)])
 
     def decode(h, t):
         b = 4 + h; xx = T["XX_%d" % h]
-        sf, fk = view("SF", h); su, uk = view("SU", h); L, R = "L%d" % t, "R%d" % t
-        tt([(b, "kt"), "MK"], [("XX", h)], xx[:], B[b][:, 128:256], T.MK[:], ALU.mult, n=128, cy=1.0)
-        mm([("XX", h), "SL"], [(b, "p")], B[b][:, 256:256 + C], xx[:], T.SL[:], n=C, cy=4.0)
-        ts([(b, "p")], [fk("y")], sf("y"), B[b][:, 256:256 + C], ZV, ALU.min, -2047.0, ALU.add)
-        ts([fk("y")], [fk("u")], sf("u"), sf("y"), MAG, ALU.add, -MAG, ALU.add)
-        if t < 3: ts([fk("u")], [uk("R")], su("R"), sf("u"), 1.0 / 4096, ALU.mult)
-        tt([fk("y"), fk("u")], [fk("t")], sf("t"), sf("y"), sf("u"), ALU.subtract)
-        if t < 3: ts([fk("t")], [uk("L")], su("L"), sf("t"), 2047.0, ALU.add)
-        lin([fk("u")], [fk(R)], sf(R), sf("u"), 1.0 / 4096)
-        lin([fk("t")], [fk(L)], sf(L), sf("t"), 1.0, 2047.0)
-
-    def count(h, n, a, b, ka, kb, m=None, km=None):
-        sf, fk = view("SF", h); sc, sk = view("SC", h)
-        f = "ne%d" % n
-        tt([ka, kb], [fk(f)], sf(f), a, b, ALU.not_equal)
-        if m is not None: tt([fk(f), km], [fk(f + "m")], sf(f + "m"), sf(f), m, ALU.mult); f = f + "m"
-        act([fk(f)], [fk("junk"), sk("D%d" % n)], sf("junk"), sf(f), accum_out=sc("D%d" % n))
+        sf, fk = view("SF", h); su, uk = view("SU", h); sh, hk = view("SH", h); L, R = "L%d" % t, "R%d" % t
+        pp = B[b][:, 256:256 + C]
+        mm(["AN", "ON"], [(b, "p")], pp, T.AN[:], T.ON[:, 0:C], True, False, n=C)
+        tt([(b, "kt"), "MK"], [("XX", h)], xx[:], B[b][:, 128:256], T.MK[:], ALU.min, n=128, cy=1.0)
+        mm([("XX", h), "SL"], [(b, "p")], pp, xx[:], T.SL[:], False, True, n=C, cy=4.0)
+        ts([(b, "p")], [fk("u")], sf("u"), pp, MAG, ALU.add, -MAG, ALU.add)
+        tt([(b, "p"), fk("u")], [hk(L)], sh(L), pp, sf("u"), ALU.subtract, cy=1.0)
+        ts([fk("u")], [hk(R)], sh(R), sf("u"), 1.0 / 4096, ALU.mult)
+        if t < 3:
+            j = slot[("SH", h)][L] * C; i = slot[("SU", h)][L] * C
+            ts([hk(L), hk(R)], [uk(L), uk(R)], T["SU_%d" % h][:, i:i + 2 * C], T["SH_%d" % h][:, j:j + 2 * C], float(CTR), ALU.add, n=64)
 
     def expand(h, ep, t):
         decode(h, t)
-        sf, fk = view("SF", h); su, uk = view("SU", h); sc, sk = view("SC", h)
+        su, uk = view("SU", h); sc, sk = view("SC", h); sh, hk = view("SH", h); sb, bk_ = view("SB", h)
+        o = 2 + h
         if t == 1:
-            votes(ep, h, [(su("L"), uk("L")), (su("R"), uk("R"))], NV2)
-            count(h, 0, sf("R1"), sf("L1"), fk("R1"), fk("L1"))
-            counts(h)
-            tt([fk("L1"), fk("R1")], [fk("DL")], sf("DL"), sf("R1"), sf("L1"), ALU.subtract)
-            vote_out(h, 2)
+            votes(ep, h, [(su("L1"), uk("L1")), (su("R1"), uk("R1"))], NV2, ("R1", "L1"))
         else:
-            ts([fk("t")], [fk("qe")], sf("qe"), sf("t"), float(Z - 2047), ALU.is_ge, float(Z), ALU.mult)
-            tt([fk("C0"), fk("qe")], [fk("C")], sf("C"), sf("C0"), sf("qe"), ALU.max)
-            vcopy([fk("C")], [uk("C")], su("C"), sf("C"))
-            votes(ep, h, [(su("L"), uk("L")), (su("R"), uk("R")), (su("C"), uk("C"))], NV3)
-            lin([sk("s2"), sk("dr1")], [sk("cinv")], sc("cinv"), sc("nh2"), sc("dr1"), n=1)
-            lin([sk("cinv")], [sk("cval")], sc("cval"), sc("cinv"), -1.0, 1.0, n=1)
-            lin([sk("s2b")], [sk("c0")], sc("c0"), sc("h2"), -16.0, 32.0, n=1)
-            lin([sk("s2b")], [sk("m0")], sc("m0"), sc("h2"), 16.0, 16.0, n=1)
-            lin([sk("cinv"), sk("m0")], [sk("c2")], sc("c2"), sc("cinv"), -BIG, sc("m0"), n=1)
-            count(h, 0, sf("R2"), sf("L2"), fk("R2"), fk("L2"))
-            count(h, 1, sf("R2"), sf("C"), fk("R2"), fk("C"))
-            counts(h)
-            vote_out(h, 3)
-
-    def coef(h, o, i, ik_, scale=1.0, sk_=None, bias=None, bk_=None):
-        sc, sk = view("SC", h)
-        R = [sk(ik_)] + ([sk(sk_)] if sk_ else []) + ([sk(bk_)] if bk_ else [])
-        lin(R, [sk(o)], sc(o), sc(i), sc(scale) if sk_ else scale, sc(bias) if bk_ else bias, n=1)
+            y = B[o][:, 448:512]; dg = T["DG_%d" % h]
+            mm([("DG", h, "q1"), hk("L1")], [(o, "xc")], y, dg[:, 128:256], sh("L1"), True, False, n=C)
+            mm([("DG", h, "q0"), hk("R1")], [(o, "xc")], y, dg[:, 0:128], sh("R1"), False, False, n=C)
+            ts([hk("L2")], [bk_("qe")], sb("qe"), sh("L2"), float(Z - CTR), ALU.is_ge, 8192.0, ALU.mult)
+            mm(["IB", bk_("qe")], [(o, "xc")], y, T.IB[:], sb("qe"), False, True, n=C)
+            ts([(o, "xc")], [uk("C")], su("C"), y, float(Z - CTR), ALU.min, float(CTR), ALU.add)
+            ts([(o, "xc")], [hk("C")], sh("C"), y, float(Z - CTR), ALU.min)
+            votes(ep, h, [(su("L2"), uk("L2")), (su("R2"), uk("R2")), (su("C"), uk("C"))], NV3, ("R2", "L2"))
 
     def last(h, ep):
         decode(h, 3)
-        sf, fk = view("SF", h); sb, bk_ = view("SB", h)
-        ts([fk("t")], [bk_("live")], sb("live"), sf("t"), float(Z - 2047), ALU.is_lt)
+        sh, hk = view("SH", h); sb, bk_ = view("SB", h)
+        ts([hk("L3")], [bk_("live")], sb("live"), sh("L3"), float(Z - CTR), ALU.is_lt)
         for kb in range(KN // 4):
-            P = (6 if h == 0 else 0) + kb if H == 2 else [6, 7, 0, 1][kb]
+            P = (6 if h == 0 else 0) + kb
             for kl in range(4):
                 k = 4 * kb + kl
                 for mp in range(H):
@@ -435,149 +455,94 @@ def rank_program(g, core, T, topo):
             b = (h * KN) // 4 + kb
             cp([(P, "lv")], [("lv", b)], T.LV[:, 512 * b:512 * b + 512], B[P][:], 512)
 
-    def last2(h, ep):
-        sf, fk = view("SF", h); sb, bk_ = view("SB", h); sc, sk = view("SC", h)
-        for n, s in ((0, None), (1, "L2"), (2, "R2"), (3, "C")):
-            if s is None: count(h, n, sf("R3"), sf("L3"), fk("R3"), fk("L3"))
-            else: count(h, n, sf("R3"), sf(s), fk("R3"), fk(s), sb("live"), bk_("live"))
-        counts(h)
-        ship(h, 0, 8)
-        coef(h, "p", "sA", "s3", "nh2", "s2")
-        coef(h, "wL", "sC", "s3", "h2", "s2b", "p", "p")
-        coef(h, "wA", "p", "p", -1.0, None, "nh2", "s2")
-        coef(h, "q", "sC", "s3", "h2", "s2b")
-        coef(h, "wC", "q", "q", -1.0, None, "h2", "s2b")
-        coef(h, "p1", "sA", "s3", "h2", "s2b")
-        coef(h, "qx", "sC", "s3", "nh2", "s2")
-        coef(h, "xL", "sC", "s3", "nh2", "s2", "p1", "p1")
-        coef(h, "xA", "p1", "p1", -1.0, None, "h2", "s2b")
-        coef(h, "xC", "qx", "qx", -1.0, None, "nh2", "s2")
-        coef(h, "k1c", "dr1", "dr1", -1.0, None, 1.0)
-        coef(h, "u", "dr2", "dr2", "dr1", "dr1")
-        coef(h, "k2", "u", "u", -1.0, None, "dr1", "dr1")
-        coef(h, "t", "sB", "s3", "k2", "k2")
-        coef(h, "bL", "xL", "xL", "k1c", "k1c", "t", "t")
-        coef(h, "bA", "xA", "xA", "k1c", "k1c")
-        coef(h, "bC", "xC", "xC", "k1c", "k1c")
-        coef(h, "bB", "t", "t", -1.0, None, "k2", "k2")
-        coef(h, "v1", "dr2", "dr2", -1.0, None, 1.0)
-        coef(h, "v2", "cval", "cval")
-
-    def weigh(h, out, terms):
-        sf, fk = view("SF", h); sc, sk = view("SC", h)
-        cur = None
-        for j, (a, c) in enumerate(terms):
-            f = "%s%d" % (out, j)
-            lin([fk(a), sk(c)], [fk(f)], sf(f), sf(a), sc(c))
-            if j:
-                n = out if j == len(terms) - 1 else "%ss%d" % (out, j)
-                tt([fk(f), fk(cur)], [fk(n)], sf(n), sf(cur), sf(f), ALU.add)
-                f = n
-            cur = f
-
     def lookups(h, ep):
-        su, uk = view("SU", h)
+        su, uk = view("SU", h); sb, bk_ = view("SB", h)
         lk = [("lv", j) for j in range(4)] + [("lvz",)]
-        b = 4 + h
-        for j, (n, l) in enumerate((("GA", "v2"), ("GB", "v3"))):
+        b = 4 + h; die = B[b][:, 320:320 + C]
+        for j, (n, l) in enumerate((("GA", "x2"), ("GB", "x3"))):
             for c in range(0, NP, CP):
-                cp(lk + [uk(l)], [(n, h, c)], T["%s_%d" % (n, h)][:, c:c + CP], T.LV[:].indirect(su(l)[:, c // 16:(c + CP) // 16]), CP, CG)
+                cp(lk + [uk(l)], [(n, h, c)], T["%s_%d" % (n, h)][:, c:c + CP], T.LV[:, 0:WW].indirect(su(l)[:, c // 16:(c + CP) // 16]), CP, CG)
+        mm(["I4", bk_("live")], [(b, "die")], die, T.I4[:], sb("live"), True, False, n=C)
+        for n in ("e2", "e3"): mm(["NI", bk_(n)], [(b, "die")], die, T.NI[:], sb(n), False, False, n=C)
+        for j, n in enumerate(("GA", "GB")):
             for i in range(16):
-                mm([("FD", i)] + [(n, h, c) for c in range(0, NP, CP)], [(b, "die")], B[b][:, 320:320 + C], T.FD[:, 128 * i:128 * i + 128], T["%s_%d" % (n, h)][:, i:NP:16], j == 0 and i == 0, j == 1 and i == 15, n=C)
+                mm([("FD", i)] + [(n, h, c) for c in range(0, NP, CP)], [(b, "die")], die, T.FD[:, 128 * i:128 * i + 128], T["%s_%d" % (n, h)][:, i:NP:16], False, j == 1 and i == 15, n=C)
 
     def ab(h, ep):
-        sf, fk = view("SF", h); sc, sk = view("SC", h)
-        iv = T.IV[:, C * h:C * h + C]
-        weigh(h, "a", [("L3", "wL"), ("L2", "wA"), ("C", "wC")])
-        weigh(h, "b", [("L3", "bL"), ("L2", "bA"), ("C", "bC"), ("R2", "bB")])
-        o = 2 + h; p = par[h]; par[h] = 1 - p
-        dsum(h, o, p)
-        buf = T["SC_%d" % h]; so = slot[("SC", h)]
-
-        def row(a, n): return buf[:, so[a]:so[a] + n]
-        ts([(o, "d")], [sk("z")], row("z0", 4), B[o][:, 384:388], 0.0, ALU.is_equal)
-        ts([sk("z")], [sk("y")], row("y0", 3), row("z1", 3), sc("z0"), ALU.subtract)
-        tt([sk("y"), sk("s3")], [sk("q3")], row("q0", 3), row("y0", 3), row("sA", 3), ALU.mult)
-        tt([sk("z"), sk("q3")], [sk("y")], row("y0", 3), row("z1", 3), row("q0", 3), ALU.subtract)
-        tt([sk("y"), sk("v0"), sk("v1"), sk("v2")], [sk("q3")], row("q0", 3), row("y0", 3), row("v0", 3), ALU.mult)
-        red([sk("q3")], [sk("dr3")], sc("dr3"), row("q0", 3))
-        tt([fk("a"), fk("R3")], [fk("m0")], sf("m0"), sf("a"), sf("R3"), ALU.subtract)
-        lin([fk("m0"), sk("dr3")], [fk("m1")], sf("m1"), sf("m0"), sc("dr3"))
-        tt([fk("m1"), fk("R3")], [fk("m2")], sf("m2"), sf("m1"), sf("R3"), ALU.add)
-        lin([fk("m2"), sk("u")], [fk("m3")], sf("m3"), sf("m2"), sc("u"))
-        tt([fk("m3"), fk("b")], [fk("bb")], sf("bb"), sf("b"), sf("m3"), ALU.add)
-        tt([fk("a"), ("IV", h)], [fk("da")], sf("da"), sf("a"), iv, ALU.subtract)
-        tt([fk("bb"), ("IV", h)], [fk("db")], sf("db"), sf("bb"), iv, ALU.subtract)
-        lin([fk("bb")], [fk("m4")], sf("m4"), sf("bb"), 4096.0)
-        tt([fk("m4"), fk("a")], [fk("ab")], sf("ab"), sf("m4"), sf("a"), ALU.add)
+        sh, hk = view("SH", h); o = 2 + h; dg = T["DG_%d" % h]
+        for y, terms in ((384, (("n0", "L2", 4), ("n2", "C", 5), ("wL", "L3", 6))), (448, (("n3", "L2", 7), ("n5", "C", 8), ("n4", "R2", 9), ("bL", "L3", 10), ("bR", "R3", 11)))):
+            for i, (c, l, j) in enumerate(terms):
+                mm([("DG", h, "c" + c), hk(l)], [(o, "xc")], B[o][:, y:y + C], dg[:, 128 * j:128 * j + 128], sh(l), i == 0, i == len(terms) - 1, n=C)
 
     def calls(h, ep):
-        sf, fk = view("SF", h); sb, bk_ = view("SB", h); su, uk = view("SU", h)
-        iv = T.IV[:, C * h:C * h + C]; b = 4 + h
-        tt([(b, "die"), fk("eq")], [fk("m1")], sf("m1"), B[b][:, 320:320 + C], sf("eq"), ALU.is_equal, cy=1.0)
-        tt([fk("m1"), bk_("live")], [fk("go")], sf("go"), sf("m1"), sb("live"), ALU.mult)
-        for n in ("a", "b"):
-            tt([fk("d" + n), fk("go")], [fk("e" + n)], sf("e" + n), sf("d" + n), sf("go"), ALU.mult)
-            tt([fk("e" + n), ("IV", h)], [fk("f" + n)], sf("f" + n), sf("e" + n), iv, ALU.add)
-            vcopy([fk("f" + n)], [uk(n)], su(n), sf("f" + n))
-
-    def pieces(h, ep):
-        sf, fk = view("SF", h); sb, bk_ = view("SB", h)
-        if ep == 1:
-            lin([fk("go")], [bk_("ng")], sb("ng"), sf("go"), -1.0, 1.0)
-            tt([fk("ab"), fk("go")], [fk("vf")], sf("vf"), sf("ab"), sf("go"), ALU.mult)
-        else:
-            lin([fk("go")], [fk("n2")], sf("n2"), sf("go"), -1.0, 1.0)
-            tt([fk("n2"), bk_("ng")], [bk_("ng")], sb("ng"), sb("ng"), sf("n2"), ALU.mult)
-            tt([fk("vf"), fk("n2")], [fk("vg")], sf("vg"), sf("vf"), sf("n2"), ALU.mult)
-            tt([fk("ab"), fk("go")], [fk("vh")], sf("vh"), sf("ab"), sf("go"), ALU.mult)
-            tt([fk("vg"), fk("vh")], [fk("vf")], sf("vf"), sf("vg"), sf("vh"), ALU.add)
-        cp([fk("vf")], [bk_("v0")], sb("v0"), sf("vf"), 64)
-        tt([fk("vf"), bk_("v0")], [fk("vr")], sf("vr"), sf("vf"), sb("v0"), ALU.subtract)
-        cp([fk("vr")], [bk_("v1")], sb("v1"), sf("vr"), 64)
-        tt([fk("vr"), bk_("v1")], [bk_("v2")], sb("v2"), sf("vr"), sb("v1"), ALU.subtract)
+        sb, bk_ = view("SB", h); su, uk = view("SU", h); sh, hk = view("SH", h); o = 2 + h; b = 4 + h
+        ts([(b, "die")], [bk_("go")], sb("go"), B[b][:, 320:320 + C], 4.0, ALU.is_equal)
+        ts([(b, "die")], [bk_("ng")], sb("ng"), B[b][:, 320:320 + C], 4.0, ALU.not_equal)
+        for n, y in (("ma", 384), ("mb", 448)): tt([(o, "xc"), bk_("go")], [hk(n)], sh(n), B[o][:, y:y + C], sb("go"), ALU.mult, cy=1.0)
+        tt([("IV", h), bk_("ng")], [hk("nv")], sh("nv"), T.IV[:, C * h:C * h + C], sb("ng"), ALU.mult)
+        for n, y in (("ma", 0), ("mb", 64)):
+            mm(["IB", hk("nv")], [(b, "ab")], B[b][:, y:y + C], T.IB[:], sh("nv"), True, False, n=C)
+            mm(["IB", hk(n)], [(b, "ab")], B[b][:, y:y + C], T.IB[:], sh(n), False, True, n=C)
+        i = slot[("SU", h)]["a"] * C
+        ts([(b, "ab")], [uk("a"), uk("b")], T["SU_%d" % h][:, i:i + 2 * C], B[b][:, 0:128], float(CTR), ALU.add, n=128)
 
     def neww(h, ep):
         t = T["W%d" % ep]
         su, uk = view("SU", h)
         wk = [("w", ep, j) for j in range(4)] + [("wg", ep), ("wz", ep)]
-        for n, l in (("GA", "a"), ("GB", "b")):
-            for c in range(0, NP, CP):
+        for c in range(0, NP, CP):
+            for n, l in (("GA", "a"), ("GB", "b")):
                 cp(wk + [uk(l)], [(n, h, c)], T["%s_%d" % (n, h)][:, c:c + CP], t[:, 0:WW].indirect(su(l)[:, c // 16:(c + CP) // 16]), CP, CG)
 
-    def neww2(h, ep):
-        out = T.W2 if ep == 1 else T.W1
+    def listw(h):
+        for j, c in enumerate(range(0, NP, 512)):
+            P = (6 if h == 0 else 0) + j
+            mm(["IB", "QT"], [(P, "nw")], B[P][:], T.IB[:], T.QT[:], True, False, n=512)
+            for n in ("GA", "GB"): mm(["HB", (n, h, c)], [(P, "nw")], B[P][:], T.HB[:], T["%s_%d" % (n, h)][:, c:c + 512], False, n == "GB", n=512)
+            ts([(P, "nw")], [("WP", h, j)], T.WP[:, h * NP + c:h * NP + c + 512], B[P][:], 8388608.0, ALU.add, -8388608.0, ALU.add, n=512)
+
+    def classw(h):
         for kb in range(KN // 4):
-            P = (6 if h == 0 else 0) + kb if H == 2 else [6, 7, 0, 1][kb]
+            P = (6 if h == 0 else 2) + kb
+            for kl in range(4):
+                mm(["IB"] + [("WP", h, j) for j in range(NP // 512)], [(P, "cw")], B[P][:, 128 * kl:128 * kl + 128], T.IB[:], T.WP[:, h * NP + 4 * kb + kl:h * NP + NP:KN])
+            b = h * KN // 4 + kb
+            cp([(P, "cw")], [("w", 2, b)], T.W2[:, 512 * b:512 * b + 512], B[P][:], 512)
+
+    def outw(h):
+        for kb in range(KN // 4):
+            P = (6 if h == 0 else 0) + kb
             mm(["IB", "QT"], [(P, "nw")], B[P][:], T.IB[:], T.QT[:], True, False, n=512)
             for n in ("GA", "GB"):
                 for kl in range(4):
                     mm(["HB"] + [(n, h, c) for c in range(0, NP, CP)], [(P, "nw")], B[P][:, 128 * kl:128 * kl + 128], T.HB[:], T["%s_%d" % (n, h)][:, 4 * kb + kl:NP:KN], False, n == "GB" and kl == 3)
             b = h * KN // 4 + kb
-            ts([(P, "nw")], [("w", 3 - ep, b)], out[:, 512 * b:512 * b + 512], B[P][:], 8388608.0, ALU.add, -8388608.0, ALU.add, n=512)
-            if ep == 2: dma("Y", [("w", 1, b)], [("yw", b)], T.yw[:, 512 * b:512 * b + 512], out[:, 512 * b:512 * b + 512])
+            ts([(P, "nw")], [("w", 1, b)], T.W1[:, 512 * b:512 * b + 512], B[P][:], 8388608.0, ALU.add, -8388608.0, ALU.add, n=512)
+            dma("Y", [("w", 1, b)], [("yw", b)], T.yw[:, 512 * b:512 * b + 512], T.W1[:, 512 * b:512 * b + 512])
 
     def kidsout(h, ep, kb):
-        sb, bk_ = view("SB", h)
+        sb, bk_ = view("SB", h); sh, hk = view("SH", h)
         b = h * KN // 4 + kb
         Pn, Pv = (6 + b % 2, b % 2) if ep == 1 else ((2, 3), (4, 5))[b % 2]
-        if ep == 1:
-            act([("w", 2, b)], [("PR", b)], T.PR[:, 512 * b:512 * b + 512], T.W2[:, 512 * b:512 * b + 512], ACT.Sign, n=512)
-            mm(["IB", "BT"], [(Pv, "vl")], B[Pv][:], T.IB[:], T.BT[:], True, False, n=512)
-            mm(["NB", ("PR", b)], [(Pv, "vl")], B[Pv][:], T.NB[:], T.PR[:, 512 * b:512 * b + 512], False, False, n=512)
         todo = [(4 * kb + kl, kl, mp) for kl in range(4) for mp in range(H)]
         for j, (k, kl, mp) in enumerate(todo):
             i = mp * KN + k
             mm([("LR", i), bk_("ng")], [(Pn, "ng")], B[Pn][:, 128 * kl + mp:128 * kl + 128:H], T.LR[:, 128 * i:128 * i + 128], sb("ng"), n=C)
+        if ep == 2: mm(["A0", "ON"], [(Pv, "vl")], B[Pv][:], T.A0[:], T.ON[:], True, False, n=512)
         for j, (k, kl, mp) in enumerate(todo):
             i = mp * KN + k
-            for n in range(3):
-                mm([("LR", i), bk_("v%d" % n)], [(Pv, "vl")], B[Pv][:, 128 * kl + mp:128 * kl + 128:H], T.LR[:, 128 * i:128 * i + 128], sb("v%d" % n),
-                   ep == 2 and n == 0, n == 2 if ep == 2 else (n == 2 and j == len(todo) - 1), n=C)
-        kt = T.KT[:, 512 * b:512 * b + 512]
-        tt([("ki", b), (Pn, "ng")], [("kt", b)], kt, T.KI[:, 512 * b:512 * b + 512], B[Pn][:], ALU.mult, n=512, cy=1.0)
-        tt([("kt", b), (Pv, "vl")], [("kt", b)], kt, kt, B[Pv][:], ALU.max if ep == 1 else ALU.add, n=512, cy=1.0)
-        if ep == 2: dma("Y", [("kt", b)], [("yk", b)], T.yk[:, 512 * b:512 * b + 512], kt)
+            for n, m in enumerate(("LR", "LB")):
+                mm([(m, i), hk(("ma", "mb")[n])], [(Pv, "vl")], B[Pv][:, 128 * kl + mp:128 * kl + 128:H], T[m][:, 128 * i:128 * i + 128], sh(("ma", "mb")[n]),
+                   ep == 1 and n == 0, n == 1 if ep == 1 else (n == 1 and j == len(todo) - 1), n=C)
+        kf = T.KF[:, 512 * b:512 * b + 512]
+        tt([("kf", b), (Pn, "ng")], [("kf", b)], kf, kf, B[Pn][:], ALU.mult, n=512, cy=1.0)
+        tt([("kf", b), (Pv, "vl")], [("kf", b)], kf, kf, B[Pv][:], ALU.add, n=512, cy=1.0)
+        if ep == 1:
+            act([("w", 2, b)], [("PR", b)], T.PR[:, 512 * b:512 * b + 512], T.W2[:, 512 * b:512 * b + 512], ACT.Sign, n=512)
+            mm(["AS", "ON"], [(Pn, "ab")], B[Pn][:], T.AS[:], T.ON[:], True, False, n=512)
+            mm(["NB", ("PR", b)], [(Pn, "ab")], B[Pn][:], T.NB[:], T.PR[:, 512 * b:512 * b + 512], False, True, n=512)
+            tt([("kf", b), (Pn, "ab")], [("kt", b)], T.KT[:, 512 * b:512 * b + 512], kf, B[Pn][:], ALU.add, n=512, cy=1.0)
+        else: dma("Y", [("kf", b)], [("yk", b)], T.yk[:, 512 * b:512 * b + 512], kf)
 
     def absent(ep, b, P):
         t = T["W%d" % ep]
@@ -585,47 +550,63 @@ def rank_program(g, core, T, topo):
         mm(["IB", "BT"], [(P, "ab")], B[P][:], T.IB[:], T.BT[:], True, False, n=512)
         mm(["NB", wk], [(P, "ab")], B[P][:], T.NB[:], t[:, 512 * b:512 * b + 512], False, True, n=512)
         if b < 4: tt([("ki", b), (P, "ab")], [("kt", b)], T.KT[:, 512 * b:512 * b + 512], T.KI[:, 512 * b:512 * b + 512], B[P][:], ALU.max, n=512, cy=1.0)
-        else: tt(["GI", (P, "ab")], ["ktg"], T.KT[:, 512 * b:512 * b + 512], T.GI[:, 512 * b - V:512 * b - V + 512], B[P][:], ALU.max, n=512, cy=1.0)
+        else: tt(["GI", (P, "ab")], [("ktg", b)], T.KT[:, 512 * b:512 * b + 512], T.GI[:, 512 * b - V:512 * b - V + 512], B[P][:], ALU.max, n=512, cy=1.0)
 
     HS = range(H)
-    for h in HS:
-        positions(1, h)
-        vote1(h)
-    for b in range(4): absent(1, b, 4 + b % 2)
-    for ep in (1, 2):
-        if ep == 2:
-            for h in HS:
-                positions(2, h)
-                vote1(h)
-            for h in HS: pieces(h, 1)
-            for h in HS:
-                for kb in range(KN // 4): kidsout(h, 1, kb)
-        for h in HS: choose(h, ep, 1)
-        for b in range(4, 7): absent(ep, b, 6 + b % 2)
-        for h in HS: expand(h, ep, 1)
-        for h in HS: choose(h, ep, 2)
-        for h in HS: expand(h, ep, 2)
-        for h in HS: choose(h, ep, 3)
-        for h in HS: last(h, ep)
-        for h in HS: last2(h, ep)
-        for h in HS: lookups(h, ep)
+
+    def each(f, *a):
         for h in HS:
-            ab(h, ep)
-            calls(h, ep)
-            neww(h, ep)
+            half[0] = h
+            f(h, *a)
+        half[0] = None
+
+    def start(h):
+        positions(h)
+        vote1(h)
+    each(start)
+    for b in range(4): absent(1, b, 4 + b % 2)
+    for b in range(4): ts([("ki", b)], [("kf", b)], T.KF[:, 512 * b:512 * b + 512], T.KI[:, 512 * b:512 * b + 512], -4097.0 * CTR, ALU.add, n=512)
+    for i in range(16):
+        lin([("LR", i)], [("LB", i)], T.LB[:, 128 * i:128 * i + 128], T.LR[:, 128 * i:128 * i + 128], 4096.0, n=128)
+    pp = {}
+
+    def vote(h, ep, t): pp[h] = choose(h, ep, t)
+
+    def table(h, ep):
+        for kb in range(KN // 4): kidsout(h, ep, kb)
+
+    def looks(h, ep):
+        ab(h, ep)
+        lookups(h, ep)
+
+    def finish(h, ep):
+        calls(h, ep)
+        neww(h, ep)
         if ep == 1:
-            neww2(0, 1)
-            ghosts(2)
-            for h in range(1, H): neww2(h, 1)
-        else:
-            for h in HS: pieces(h, 2)
-            for h in HS:
-                for kb in range(KN // 4): kidsout(h, 2, kb)
-            for h in HS: neww2(h, 2)
+            listw(h)
+            vote1(h)
+            classw(h)
+            if h == 0: ghosts(2)
+    for ep in (1, 2):
+        if ep == 2: each(table, 1)
+        each(vote, ep, 1)
+        for b in range(4, 7): absent(ep, b, 6 + b % 2)
+        each(expand, ep, 1)
+        each(vote, ep, 2)
+        each(lambda h: drops(h, 2, pp[h]))
+        each(expand, ep, 2)
+        each(vote, ep, 3)
+        each(lambda h: drops(h, 3, pp[h]))
+        each(last, ep)
+        each(looks, ep)
+        each(finish, ep)
+        if ep == 2:
+            each(table, 2)
+            each(outw)
 
     n = len(nodes); pred = [set() for _ in range(n)]
     lw = {}; lr = {}; bp = {}
-    for i, (q, R, W, _e, _c, _l) in enumerate(nodes):
+    for i, (q, R, W, _e, _c, _l, _h) in enumerate(nodes):
         for k in R:
             if k in lw: pred[i].add(lw[k])
         for k in W:
@@ -648,6 +629,8 @@ def rank_program(g, core, T, topo):
     for i in range(n - 1, -1, -1):
         m = max([prio[j] for j in succ[i]] or [0.0])
         prio[i] = nodes[i][4] + nodes[i][5] + m + (WAKE if nodes[i][0] != "P" else 0.0)
+    for i in range(n):
+        if nodes[i][6] == 0: prio[i] += LEAD
     left = [len(p) for p in pred]; est = [0.0] * n; ready = {q: [] for q in eng}; free = {q: 0.0 for q in eng}; order = []
 
     def offer(i):

import numpy as np
from concourse.bass import DstId, RemoteDMATransfer
from concourse.mybir import AluOpType as ALU, AxisListType, ActivationFunctionType as ACT
import comms_topo

V, X = 2048, 512
H = 2
KN = 16 // H
NP = V // H
C = 128 // H
NC = NP // 128
WW = 3600
Z = 3584
BIG = 16777216.0
ZV = 4097.0 * Z
CTR = 1792
MAG = 51539607552.0
NV2 = (6, 5)
NV3 = (6, 5, 5)
CUTS = {1: (1,), 2: (1, 2), 3: (2, 3)}
CP = 512
VC = 4
CY, PE, CG, WAKE, RLAT, RCOL, DLAT, SELF, LEAD = 0.83e-3, 0.6e-3, 1.56, 0.08, 2.2, 0.004, 2.5, 0.06, 2.5

SF = 2; SU = 9; SB = 6; SC = 64; SH = 10
SCRATCH = {
    "W1": ("sbuf", [128, WW], "bfloat16"), "W2": ("sbuf", [128, WW], "bfloat16"),
    "KT": ("sbuf", [128, WW], "float32"), "KI": ("sbuf", [128, V], "int32"),
    "WP": ("sbuf", [128, V], "bfloat16"), "GI": ("sbuf", [128, 3 * X], "float32"), "PR": ("sbuf", [128, V], "bfloat16"),
    "LV": ("sbuf", [128, WW], "bfloat16"), "KF": ("sbuf", [128, V], "float32"),
    "LB": ("sbuf", [128, 2048], "bfloat16"), "LR": ("sbuf", [128, 2048], "bfloat16"), "FD": ("sbuf", [128, 2048], "bfloat16"),
    "IC": ("sbuf", [128, 128], "int32"), "ID": ("sbuf", [128, 128], "int32"), "IM": ("sbuf", [128, 128], "int32"), "IS": ("sbuf", [128, 64], "int32"),
    "IV": ("sbuf", [128, 128], "float16"), "IP": ("sbuf", [128, 2], "int32"), "IQ": ("sbuf", [128, 4], "int32"), "PG": ("sbuf", [128, 12], "float32"), "CI": ("sbuf", [128, 16], "int32"), "CM": ("sbuf", [128, 16], "float32"),
    "IB": ("sbuf", [128, 128], "bfloat16"), "NB": ("sbuf", [128, 128], "bfloat16"), "HB": ("sbuf", [128, 128], "bfloat16"), "NI": ("sbuf", [128, 128], "bfloat16"), "I4": ("sbuf", [128, 128], "bfloat16"),
    "A0": ("sbuf", [128, 128], "bfloat16"), "AN": ("sbuf", [128, 128], "bfloat16"), "AS": ("sbuf", [128, 128], "bfloat16"), "NT": ("sbuf", [128, 128], "bfloat16"),
    "ON": ("sbuf", [128, 512], "bfloat16"), "DC": ("sbuf", [128, 384], "bfloat16"),
    "BT": ("sbuf", [128, 512], "bfloat16"), "QT": ("sbuf", [128, 512], "bfloat16"),
    "CB": ("sbuf", [128, 384], "bfloat16"), "F": ("sbuf", [128, 128], "float16"), "E": ("sbuf", [128, 128], "float16"),
    "GQ": ("sbuf", [128, 128], "bfloat16"), "MK": ("sbuf", [128, 128], "float32"), "SL": ("sbuf", [128, C], "float32"),
    "T1": ("sbuf", [128, 128], "float32"), "T2": ("sbuf", [128, 384], "float32"), "T3": ("sbuf", [128, 128], "float32"),
}
for _j in range(7): SCRATCH["IT%d" % _j] = ("sbuf", [128, 128], "int32")
for _h in range(H):
    for _n, _w, _t in (("G", NP, "float32"), ("M0", NP, "bfloat16"), ("M1", NP, "bfloat16"), ("M2", NP, "bfloat16"), ("RW", NP, "bfloat16"),
                       ("GA", NP, "bfloat16"), ("GB", NP, "bfloat16"), ("SND0", 392, "float16"), ("SND1", 392, "float16"), ("LND0", 3 * 392, "float16"),
                       ("LND1", 3 * 392, "float16"), ("OH", 384, "bfloat16"), ("OT", 128, "float32"), ("XX", 128, "float32"),
                       ("SF", SF * C, "float32"), ("SU", SU * C, "uint16"), ("SB", SB * C, "bfloat16"), ("SH", SH * C, "float16"), ("DG", 12 * 128, "bfloat16"),
                       ("JK", 16, "float32"), ("SC", SC, "float32")):
        SCRATCH["%s_%d" % (_n, _h)] = ("sbuf", [128, _w], _t)
for _b in range(8):
    SCRATCH["B%d" % _b] = ("psum", [128, 512], "float32")
SEMAPHORES = ["cV", "cS", "cP", "cG"] + ["d%d" % i for i in range(44)] + ["a%d" % i for i in range(34)] + ["l%d" % i for i in range(34)]


def rank_program(g, core, T, topo):
    rank = T.rank_of(core)
    if rank is None:
        return
    eng = {"V": g.vector, "S": g.scalar, "P": g.tensor, "G": g, "Y": g.sync}
    cnt = {}; known = {q: {} for q in eng}; wr = {}; rd = {}; bank = {}; snap = {}; nd = [0, 0]; half = [None]
    nodes = []

    def put(d, k, s, v):
        e = d.setdefault(k, {}); e[s] = max(e.get(s, 0), v)

    def bk(k):
        return k[0] if isinstance(k, tuple) and isinstance(k[0], int) else None

    def waits(q, R, W):
        own = "c" + q; need = {}
        for k in R:
            for s, v in wr.get(k, {}).items(): need[s] = max(need.get(s, 0), v)
        for k in W:
            for d in (wr, rd):
                for s, v in d.get(k, {}).items():
                    if s != own or q != "P": need[s] = max(need.get(s, 0), v)
        for k in list(R) + list(W):
            if bk(k) is not None:
                for s, v in bank.get(bk(k), {}).items():
                    if s != own: need[s] = max(need.get(s, 0), v)
        kn = known[q]
        for s in sorted((s for s, v in need.items() if kn.get(s, 0) < v), key=lambda s: s == own):
            v = need[s]
            if kn.get(s, 0) >= v: continue
            eng[q].wait_ge(T.sem[s], v)
            kn[s] = v
            for s2, v2 in snap.get((s, v), {}).items(): kn[s2] = max(kn.get(s2, 0), v2)

    def mark(R, W, s, v):
        for k in R: put(rd, k, s, v)
        for k in W: put(wr, k, s, v)
        for k in list(R) + list(W):
            if bk(k) is not None: put(bank, bk(k), s, v)

    def done(q, R, W, i):
        s = "c" + q; cnt[s] = cnt.get(s, 0) + 1
        i.then_inc(T.sem[s], 1)
        snap[(s, cnt[s])] = dict(known[q])
        mark(R, W, s, cnt[s])

    def node(q, R, W, emit, cost, lat=0.0):
        nodes.append([q, list(R), list(W), emit, cost, lat, half[0]])

    def op(q, R, W, make, n=64, cy=1.0):
        cost = 0.06 + max(64, n * cy) * CY if q != "P" else cy * max(64, n) * PE
        R = list(R); W = list(W)

        def emit(q):
            waits(q, R, W)
            done(q, R, W, make(eng[q], q))
        node(q, R, W, emit, cost)

    def dma(q, R, W, out, in_):
        s = "d%d" % nd[0]; nd[0] += 1

        def emit(q):
            waits(q, R, W)
            eng[q].dma_start(out, in_).then_inc(T.sem[s], 16)
            cnt[s] = 16; snap[(s, 16)] = dict(known[q]); mark(R, W, s, 16)
        node(q, R, W, emit, 0.06, DLAT)

    peers = [T.cores[(rank + d) % 4] for d in (1, 2, 3)]
    ids = []; mask = 0xFFFF
    for p in peers:
        rid, pid = topo.addr(p)[:2]
        ids.append(DstId(rid=rid, pnc=pid)); mask &= topo.mask(core, p)

    def send(R, W, src, dsts):
        a, l = "a%d" % nd[1], "l%d" % nd[1]; nd[1] += 1
        n = bin(mask).count("1")

        def emit(q):
            waits("G", R, ())
            g.remote_dma_fused([RemoteDMATransfer(dst_ids=ids, dma_engine_mask=mask, remote_sem=T.sem[a], srcs=[src], dsts=dsts)], local_sem=T.sem[l])
            cnt[a] = 3 * n; cnt[l] = n
            mark(R, (), l, n); snap[(l, n)] = dict(known["G"])
            for k in W: wr[k] = {a: 3 * n}
        node("G", R, W, emit, 0.6, RLAT + RCOL * src.shape[1])

    def ts(R, W, o, i, s1, op0, s2=None, op1=None, n=64, cy=1.0):
        if op1 is None: op("V", R, W, lambda e, q: e.tensor_scalar(o, i, s1, None, op0), n, cy)
        else: op("V", R, W, lambda e, q: e.tensor_scalar(o, i, s1, s2, op0, op1), n, cy)

    def tt(R, W, o, a, b, f, n=64, cy=2.0): op("V", R, W, lambda e, q: e.tensor_tensor(o, a, b, f), n, cy)
    def red(R, W, o, i, n=64): op("V", R, W, lambda e, q: e.tensor_reduce(o, i, AxisListType.X, ALU.max), n)
    def redn(R, W, o, i, n=64): op("V", R, W, lambda e, q: e.tensor_reduce(o, i, AxisListType.X, ALU.max, negate=True), n)
    def vcopy(R, W, o, i, n=64): op("V", R, W, lambda e, q: e.tensor_copy(o, i), n)
    def fill(W, o, c, n=64): op("V", (), W, lambda e, q: e.memset(o, c), n)
    def mm(R, W, o, l, r, st=True, sp=True, n=128, cy=1.0): op("P", R, W, lambda e, q: e.matmul(o, l, r, st, sp), n, cy)
    def act(R, W, o, i, f=ACT.Copy, n=64, cy=1.0, **kw): op("S", R, W, lambda e, q: e.activation(o, i, f, **kw), n, cy)

    def iota(W, o, pat, base, ch, n, **kw): op("G", (), W, lambda e, q: e.iota(o, pat, base, ch, **kw), 2 * n)

    def cp(R, W, o, i, n, cy=1.0): op("VS", R, W, lambda e, q: e.tensor_copy(o, i) if q == "V" else e.activation(o, i, ACT.Copy), n, cy)

    def lin(R, W, o, i, scale, bias=None, n=64):
        def make(e, q):
            if bias is None: return e.tensor_scalar(o, i, scale, None, ALU.mult) if q == "V" else e.activation(o, i, ACT.Copy, scale=scale)
            return e.tensor_scalar(o, i, scale, bias, ALU.mult, ALU.add) if q == "V" else e.activation(o, i, ACT.Identity, scale=scale, bias=bias)
        op("VS", R, W, make, n)

    def hot(R, W, o, i, bias, n):
        op("VS", R, W, lambda e, q: e.tensor_scalar(o, i, bias, 0.0, ALU.add, ALU.max) if q == "V" else e.activation(o, i, ACT.Relu, bias=bias), n)
    B = [T["B%d" % b] for b in range(8)]
    slot = {}

    def arr(kind, h, name):
        d = slot.setdefault((kind, h), {})
        if name not in d: d[name] = len(d)
        w = 1 if kind == "SC" else C
        j = d[name] * w
        return T["%s_%d" % (kind, h)][:, j:j + w]

    def view(kind, h):
        return (lambda n: arr(kind, h, n)), (lambda n: (kind, h, n))

    for b in range(4):
        dma("YS"[b % 2], (), [("w", 1, b)], T.W1[:, 512 * b:512 * b + 512], T.w[:, 512 * b:512 * b + 512])
    for b in range(4):
        dma("Y", (), [("ki", b)], T.KI[:, 512 * b:512 * b + 512], T.kids[:, 512 * b:512 * b + 512])
    iota(["IC"], T.IC[:], [[1, 128]], 0, 0, 128)
    iota(["ID"], T.ID[:], [[1, 128]], 128, -1, 128)
    iota(["IP"], T.IP[:, 0:2], [[0, 2]], 0, 1, 32)

    def ghosts(ep):
        t = T["W%d" % ep]
        send([("w", ep, 0)], [("wg", ep)], t[:, 0:X], [t[:, V + (d - 1) * X:V + d * X] for d in (1, 2, 3)])
    ghosts(1)
    iota(["IM"], T.IM[:], [[1, 128]], 0, KN, 128)
    iota(["IS"], T.IS[:, 0:C], [[-H, C]], 0, 1, C)
    iota(["CI"], T.CI[:], [[1, 16]], 0, 0, 32)
    iota(["GI"], T.GI[:], [[4097, 3 * X]], V * 4097, 0, 3 * X, allow_small_or_imprecise_dtypes=True)

    LH = {1: 0, 2: 1, 4: 2}[H]; LK = 4 - LH
    IT = [T["IT%d" % j] for j in range(7)]
    ts(["ID"], ["IB"], T.IB[:], T.ID[:], 128.0, ALU.is_equal, n=128)
    fill(["BT"], T.BT[:], BIG, n=256)
    fill(["ON"], T.ON[:], 1.0, n=256)
    lin(["IB"], ["NB"], T.NB[:], T.IB[:], -BIG, n=128)
    ts(["ID"], ["IT0"], IT[0][:], T.ID[:], KN - 1, ALU.bitwise_and, n=128)
    ts(["IT0"], ["F"], T.F[:], IT[0][:], 0.0, ALU.is_equal, 64.0, ALU.mult, n=128)
    ts(["IP"], ["IQ0"], T.IQ[:, 0:1], T.IP[:, 0:1], 4, ALU.arith_shift_right)
    ts(["IP"], ["IQ1"], T.IQ[:, 1:2], T.IP[:, 1:2], 15, ALU.bitwise_and)
    vcopy(["IQ0", "IQ1"], ["PG"], T.PG[:, 0:2], T.IQ[:, 0:2])
    ts(["IC"], ["IT1"], IT[1][:], T.IC[:], 4, ALU.arith_shift_right, n=128)
    ts(["IT1", "PG"], ["GQ"], T.GQ[:], IT[1][:], T.PG[:, 0:1], ALU.is_equal, n=128)
    lin(["GQ"], ["T1"], T.T1[:], T.GQ[:], BIG, -BIG, n=128)
    ts(["IC"], ["IT2"], IT[2][:], T.IC[:], 15, ALU.bitwise_and, n=128)
    for s in range(3):
        ts(["IT2"], [("T2", s)], T.T2[:, 128 * s:128 * s + 128], IT[2][:], -1.0, ALU.mult, 15.0 + (32.0, 0.0, 16.0)[s], ALU.add, n=128)
        tt(["T1", ("T2", s)], [("CB", s)], T.CB[:, 128 * s:128 * s + 128], T.T1[:], T.T2[:, 128 * s:128 * s + 128], ALU.add, n=128)
    CBK = [("CB", 0), ("CB", 1), ("CB", 2)]
    for s in range(3): fill([("DC", s)], T.DC[:, 128 * s:128 * s + 128], (-16.0, 0.0, 16.0)[s], n=64)
    DCK = [("DC", s) for s in range(3)]
    fill(["NT"], T.NT[:], -BIG, n=64)
    ts(["IM"], ["IT3"], IT[3][:], T.IM[:], LK, ALU.arith_shift_right, H - 1, ALU.bitwise_and, n=128)
    ts(["IT3"], ["MK"], T.MK[:], IT[3][:], 0.0, ALU.is_equal, ZV, ALU.mult, n=128)
    ts(["IS"], ["IT4"], IT[4][:, 0:C], T.IS[:, 0:C], LH, ALU.arith_shift_right)
    ts(["IT4"], ["SL"], T.SL[:], IT[4][:, 0:C], 0.0, ALU.is_equal)
    lin(["IB"], ["NI"], T.NI[:], T.IB[:], -1.0, n=128)
    lin(["IB"], ["I4"], T.I4[:], T.IB[:], 4.0, n=128)
    ts(["F"], ["T3"], T.T3[:], T.F[:], 1.0 / 64, ALU.mult, n=128)
    tt(["T3", "GQ"], ["E"], T.E[:], T.T3[:], T.GQ[:], ALU.mult, n=128)
    for j in range(3): ts(["IP"], [("PC", j)], T.PG[:, 4 + j:5 + j], T.IP[:, 0:1], float(j), ALU.is_equal, (4096.0 * CTR, float(CTR), BIG)[j], ALU.mult)
    tt([("PC", 0), ("PC", 1)], ["P1"], T.PG[:, 7:8], T.PG[:, 4:5], T.PG[:, 5:6], ALU.add)
    tt(["P1", ("PC", 2)], ["P2"], T.PG[:, 8:9], T.PG[:, 7:8], T.PG[:, 6:7], ALU.add)
    ts(["ON", "P1"], ["A0"], T.A0[:], T.ON[:, 0:128], T.PG[:, 7:8], ALU.mult)
    ts(["ON", "P1"], ["AN"], T.AN[:], T.ON[:, 0:128], T.PG[:, 7:8], ALU.mult, -1.0, ALU.mult)
    ts(["ON", "P2"], ["AS"], T.AS[:], T.ON[:, 0:128], T.PG[:, 8:9], ALU.mult)
    for ep in (1, 2): fill([("wz", ep)], T["W%d" % ep][:, Z:WW], 0.0)
    fill(["ktz"], T.KT[:, Z:WW], BIG)
    ts(["IQ1"], ["IQ2"], T.IQ[:, 2:3], T.IQ[:, 1:2], KN - 1, ALU.bitwise_and)
    ts(["IQ1"], ["IQ3"], T.IQ[:, 3:4], T.IQ[:, 1:2], LK, ALU.arith_shift_right)
    ts(["IQ2"], ["PG2"], T.PG[:, 2:3], T.IQ[:, 2:3], 128.0, ALU.mult)
    tt(["PG2", "IQ3"], ["PG3"], T.PG[:, 3:4], T.PG[:, 2:3], T.IQ[:, 3:4], ALU.add)
    for h in range(H):
        ts(["IC"], [("IT", 5 + h)], IT[5 + h][:, 0:C], T.IC[:, 0:C], float(H), ALU.mult, float(h * KN * 128 - CTR), ALU.add)
        ts([("IT", 5 + h), "PG3"], [("IV", h)], T.IV[:, C * h:C * h + C], IT[5 + h][:, 0:C], T.PG[:, 3:4], ALU.add)
    ts(["CI", "PG"], ["CM"], T.CM[:], T.CI[:], T.PG[:, 1:2], ALU.is_equal)
    fill([("lvz",)], T.LV[:, V:WW], 0.0, n=(WW - V) // 2)
    fill(["QT"], T.QT[:], -0.25, n=256)
    lin(["IB"], ["HB"], T.HB[:], T.IB[:], 0.5, n=128)
    for h in range(H):
        sc, sk = view("SC", h)
        slot[("SC", h)] = {("D%d" % n): n for n in range(8)}
        for n in ["%s%d" % (a, j) for a, m in (("r", 3), ("s", 6), ("f", 6), ("p", 6), ("n", 6)) for j in range(m)]: sc(n)
        slot[("SH", h)] = {n: j for j, n in enumerate(("L1", "R1", "L2", "R2", "L3", "R3", "C", "ma", "mb", "nv"))}
        slot[("SU", h)] = {n: j for j, n in enumerate(("L1", "R1", "L2", "R2", "C", "x2", "x3", "a", "b"))}
        fill([sk("D%d" % n) for n in range(8)], T["SC_%d" % h][:, 0:8], 0.0)
        fill([sk("f1")], sc("f1"), 0.0)
    for i in range(16):
        act(["GQ", "CM"], [("LR", i)], T.LR[:, 128 * i:128 * i + 128], T.GQ[:], scale=T.CM[:, i:i + 1], n=128)
    for i in range(16):
        act(["IB", "CM"], [("FD", i)], T.FD[:, 128 * i:128 * i + 128], T.IB[:], scale=T.CM[:, i:i + 1], n=128)

    def row(h, a, n):
        j = slot[("SC", h)][a]
        return T["SC_%d" % h][:, j:j + n]

    def positions(h):
        for b in range(NP // 512):
            P = (2 if h else 6) + b
            n = 512 // KN
            for k in range(KN):
                cl = (h * KN + k)
                mm(["IB", ("w", 1, cl // 4)], [(P, "wp")], B[P][:, k:512:KN], T.IB[:], T.W1[:, 128 * cl + n * b:128 * cl + n * b + n], n=n)
            cp([(P, "wp")], [("WP", h, b)], T.WP[:, h * NP + 512 * b:h * NP + 512 * b + 512], B[P][:], 512)

    par = [0] * H

    def ship(h, a, b, head):
        p = par[h]; sn = T["SND%d_%d" % (p, h)]; ln = T["LND%d_%d" % (p, h)]
        lo, hi = (0 if head else 8 + 128 * a), 8 + 128 * b
        vcopy([(h, "o1")], [("SV", h, p, a)], sn[:, 8 + 128 * a:hi], B[h][:, 128 * a:128 * b], n=128 * (b - a))
        R = [("SV", h, p, a)] + ([("SD", h, p)] if head else []) + ([("SC", h, "dr1")] if b == 3 else [])
        send(R, [("LD", h, p, s) for s in range(a, b)] + ([("LD", h, p, "d")] if head else []), sn[:, lo:hi], [ln[:, 392 * d + lo:392 * d + hi] for d in range(3)])

    def stage1(h, s, src, key, c, st, sp, rhs="IB"):
        mm([rhs] + key, [(h, "o1")], B[h][:, 128 * s:128 * s + 128], src[:, 128 * c:128 * c + 128], T[rhs][:], st, sp)

    def vote1(h):
        w = T.WP[:, h * NP:h * NP + NP]
        for c in range(NC): stage1(h, 0, w, [("WP", h, c // 4)], c, c == 0, c == NC - 1)
        ship(h, 0, 1, False)

    def vgather(R, W, m, win, l, w, n): op("V", R, W, lambda e, q: e.tensor_tensor(m, win.indirect(l), w, ALU.min), n, CG)

    def votes(ep, h, lists, nv, apart):
        win = T["W%d" % ep][:, 0:WW]; p = par[h]
        wk = [("w", ep, b) for b in range(4)] + [("wg", ep), ("wz", ep)]
        wp = T.WP[:, h * NP:h * NP + NP]
        for s, (l, lk) in enumerate(lists):
            n = nv[s]; m = T["M%d_%d" % (s, h)]; rw = T["RW_%d" % h]
            for c in range(n, NC, 4):
                e = min(c + 4, NC); k = 128 * (e - c); rk = [("RW", h, j) for j in range(c, e)]
                act(wk + [lk], rk, rw[:, 128 * c:128 * e], win.indirect(l[:, 8 * c:8 * e]), n=k, cy=CG)
                P = 6 + h
                mm(["IB"] + [("WP", h, j) for j in sorted({c // 4, (e - 1) // 4})], [(P, "df")], B[P][:, 0:k], T.IB[:], wp[:, 128 * c:128 * e], True, False, n=k)
                mm(["NI"] + rk, [(P, "df")], B[P][:, 0:k], T.NI[:], rw[:, 128 * c:128 * e], False, True, n=k)
                act([(P, "df")], [("M", h, s, j) for j in range(c, e)], m[:, 128 * c:128 * e], B[P][:, 0:k], ACT.Relu, n=k)
            for c in range(0, n, VC):
                e = min(c + VC, n)
                vgather(wk + [lk] + [("WP", h, j) for j in sorted({c // 4, (e - 1) // 4})], [("M", h, s, j) for j in range(c, e)],
                        m[:, 128 * c:128 * e], win, l[:, 8 * c:8 * e], wp[:, 128 * c:128 * e], 128 * (e - c))
            todo = [(wp, [("WP", h, c // 4)], c, "IB") for c in range(n, NC)] + [(m, [("M", h, s, c)], c, "IB") for c in range(n)] \
                + [(m, [("M", h, s, c)], c, "NI") for c in range(n, NC)]
            for j, (src, key, c, r) in enumerate(todo): stage1(h, s, src, key, c, j == 0, j == len(todo) - 1, r)
            cuts = CUTS[len(lists)]
            if s + 1 in cuts:
                a = max([0] + [k for k in cuts if k <= s])
                if a == 0: distance(h, *apart)
                ship(h, a, s + 1, a == 0)

    def distance(h, a, b):
        sh, hk = view("SH", h); sf, fk = view("SF", h); sc, sk = view("SC", h); o = 4 + h; p = par[h]
        df = B[o][:, 448:512]
        mm(["IB", hk(a)], [(o, "ne")], df, T.IB[:], sh(a), True, False, n=C)
        mm(["NI", hk(b)], [(o, "ne")], df, T.NI[:], sh(b), False, True, n=C)
        act([(o, "ne")], [fk("junk"), sk("D0")], sf("junk"), df, ACT.Abs, scale=1.0 / 64, accum_out=sc("D0"))
        vcopy([sk("D%d" % n) for n in range(8)], [("SD", h, p)], T["SND%d_%d" % (p, h)][:, 0:8], T["SC_%d" % h][:, 0:8])

    def dsum(h, p):
        ln = T["LND%d_%d" % (p, h)]; o = 4 + h
        mm(["E", ("SD", h, p)], [(o, "d")], B[o][:, 384:392], T.E[:], T["SND%d_%d" % (p, h)][:, 0:8], True, False, n=8)
        for d in range(3): mm(["E", ("LD", h, p, "d")], [(o, "d")], B[o][:, 384:392], T.E[:], ln[:, 392 * d:392 * d + 8], False, d == 2, n=8)

    def stage2(h, ns):
        p = par[h]; par[h] = 1 - p
        ln = T["LND%d_%d" % (p, h)]; sn = T["SND%d_%d" % (p, h)]
        o = 2 + h; w = 128 * ns
        mm(CBK + ["IB"], [(o, "o2")], B[o][:, 0:w], T.IB[:], T.CB[:, 0:w], True, False, n=w)
        if ns == 3:
            mm(DCK + [("DG", h, "q1")], [(o, "o2")], B[o][:, 0:w], T["DG_%d" % h][:, 128:256], T.DC[:], False, False, n=w)
            mm(["NT", ("DG", h, "dr")], [(o, "o2")], B[o][:, 256:384], T["DG_%d" % h][:, 256:384], T.NT[:], False, False, n=128)
        for a, e in zip((0,) + CUTS[ns], CUTS[ns]):
            x, y = 128 * a, 128 * e
            mm(["F", ("SV", h, p, a)], [(o, "o2")], B[o][:, x:y], T.F[:], sn[:, 8 + x:8 + y], False, False, n=y - x)
            for d in range(3):
                mm(["F"] + [("LD", h, p, s) for s in range(a, e)], [(o, "o2")], B[o][:, x:y], T.F[:], ln[:, 392 * d + 8 + x:392 * d + 8 + y], False, d == 2 and e == ns, n=y - x)
        return p

    def onehot(h, ns):
        oh = T["OH_%d" % h]; b = 4 + h
        for s in range(ns): mm([("OH", h), "IB"], [(b, "ot")], B[b][:, 0:128], oh[:, 128 * s:128 * s + 128], T.IB[:], s == 0, s == ns - 1)
        cp([(b, "ot")], [("OT", h)], T["OT_%d" % h][:], B[b][:, 0:128], 128)

    def diag(h, name, j, col, ck):
        d = T["DG_%d" % h][:, 128 * j:128 * j + 128]
        op("VS", ["IB"] + ck, [("DG", h, name)], lambda e, q: e.tensor_scalar(d, T.IB[:], col, None, ALU.mult) if q == "V" else e.activation(d, T.IB[:], ACT.Copy, scale=col), 96)
        return d

    def choose(h, ep, t):
        ns = t; o = 2 + h; b = 4 + h
        p = stage2(h, ns)
        sc, sk = view("SC", h); su, uk = view("SU", h); sh, hk = view("SH", h); sb, bk_ = view("SB", h)
        oh = T["OH_%d" % h]; ot = T["OT_%d" % h]
        x = B[o][:, 384:448]
        if t == 1:
            red([(o, "o2")], [sk("r0")], sc("r0"), B[o][:, 0:128], 128)
            ts([(o, "o2"), sk("r0")], [("OH", h)], oh[:, 0:128], B[o][:, 0:128], sc("r0"), ALU.is_equal, n=128)
            onehot(h, 1)
        else:
            for s in range(ns): redn([(o, "o2")], [sk("r%d" % s)], sc("r%d" % s), B[o][:, 128 * s:128 * s + 128], 128)
            if t == 2:
                ts([sk("r0"), sk("r1")], [sk("bias")], sc("bias"), sc("r1"), sc("r0"), ALU.min, 1.0, ALU.add)
                ts([sk("r0"), sk("r1")], [sk("f2")], sc("f2"), sc("r1"), sc("r0"), ALU.is_lt)
                ts([sk("r0"), sk("r1")], [sk("f0")], sc("f0"), sc("r1"), sc("r0"), ALU.is_gt)
                lists = [("f0", "q0", 0, "L1"), ("f2", "q1", 1, "R1")]
            else:
                ts([sk("r0"), sk("r1")], [sk("m")], sc("m"), sc("r1"), sc("r0"), ALU.min)
                ts([sk("m"), sk("r2")], [sk("bias")], sc("bias"), sc("r2"), sc("m"), ALU.min, 1.0, ALU.add)
                ts([sk("bias")] + [sk("r%d" % s) for s in range(3)], [sk("s%d" % s) for s in range(3)], row(h, "s0", 3), row(h, "r0", 3), sc("bias"), ALU.subtract, -1.0, ALU.is_equal)
                lists = [("s0", "q0", 0, "L2"), ("s1", "q1", 1, "R2"), ("s2", "q2", 3, "C")]
            hot([(o, "o2"), sk("bias")], [("OH", h)], oh[:, 0:128 * ns], B[o][:, 0:128 * ns], sc("bias"), 128 * ns)
            onehot(h, ns)
            ds = [diag(h, q, j, sc(f), [sk(f)]) for f, q, j, l in lists]
            for i, (f, q, j, l) in enumerate(lists):
                mm([("DG", h, q), hk(l)], [(o, "xc")], x, ds[i], sh(l), i == 0, i == ns - 1, n=C)
            xn = "x%d" % t
            ts([(o, "xc")], [uk(xn)], su(xn), x, float(CTR), ALU.add)
            G = T["G_%d" % h]
            kk = [("kt", j) for j in range(4)] + [("ktg", j) for j in (4, 5, 6)] + ["ktz", uk(xn)]
            xl = su(xn)
            for c in range(0, NP, CP):
                cp(kk, [("G", h, c)], G[:, c:c + CP], T.KT[:, 0:WW].indirect(xl[:, c // 16:(c + CP) // 16]), CP, CG)
            tt([(o, "xc"), ("IV", h)], [bk_("e%d" % t)], sb("e%d" % t), x, T.IV[:, C * h:C * h + C], ALU.is_equal, cy=1.0)
        for k in range(KN):
            if t == 1:
                cl = h * KN + k
                mm([("kt", cl // 4), ("OT", h)], [(b, "kt")], B[b][:, 128 + k:256:KN], T.KT[:, 128 * cl:128 * cl + 128], ot[:, k:128:KN], n=64, cy=4.0)
            else:
                mm([("G", h, c) for c in range(0, NP, CP)] + [("OT", h)], [(b, "kt")], B[b][:, 128 + k:256:KN], T["G_%d" % h][:, k:NP:KN], ot[:, k:128:KN], n=64, cy=4.0)
        return p

    def drops(h, t, p):
        sc, sk = view("SC", h); b = 4 + h
        dsum(h, p)
        if t == 2:
            ts([(b, "d")], [sk("dr1")], sc("dr1"), B[b][:, 384:385], 0.0, ALU.is_equal)
            diag(h, "dr", 2, sc("dr1"), [sk("dr1")])
            cp([sk("f2")], [sk("f3")], sc("f3"), sc("f2"), 1)
            lin([sk("dr1"), sk("f0")], [sk("f5")], sc("f5"), sc("dr1"), -1.0, sc("f0"), n=1)
        else:
            ts([(b, "d"), sk("dr1")], [sk("bR")], sc("bR"), B[b][:, 384:385], 0.0, ALU.is_equal, sc("dr1"), ALU.mult)
            lin([sk("bR"), sk("dr1")], [sk("f4")], sc("f4"), sc("bR"), -1.0, sc("dr1"), n=1)
            cp([sk("s%d" % j) for j in range(3)], [sk("s%d" % j) for j in range(3, 6)], row(h, "s3", 3), row(h, "s0", 3), 3)
            F6 = [sk("f%d" % j) for j in range(6)]; P6 = [sk("p%d" % j) for j in range(6)]; N6 = [sk("n%d" % j) for j in range(6)]
            tt(F6 + [sk("s%d" % j) for j in range(6)], P6, row(h, "p0", 6), row(h, "s0", 6), row(h, "f0", 6), ALU.mult, n=6)
            tt(F6 + P6, N6, row(h, "n0", 6), row(h, "f0", 6), row(h, "p0", 6), ALU.subtract, n=6)
            for j, n in ((0, "wL"), (3, "bL")):
                act(P6[j:j + 3], [sk("junk%d" % j), sk(n)], T["JK_%d" % h][:, 4 * j:4 * j + 3], row(h, "p%d" % j, 3), accum_out=sc(n), n=3)
            for j, n in enumerate(("n0", "n2", "wL", "n3", "n5", "n4", "bL", "bR")): diag(h, "c" + n, 4 + j, sc(n), [sk(n)])

    def decode(h, t):
        b = 4 + h; xx = T["XX_%d" % h]
        sf, fk = view("SF", h); su, uk = view("SU", h); sh, hk = view("SH", h); L, R = "L%d" % t, "R%d" % t
        pp = B[b][:, 256:256 + C]
        mm(["AN", "ON"], [(b, "p")], pp, T.AN[:], T.ON[:, 0:C], True, False, n=C)
        tt([(b, "kt"), "MK"], [("XX", h)], xx[:], B[b][:, 128:256], T.MK[:], ALU.min, n=128, cy=1.0)
        mm([("XX", h), "SL"], [(b, "p")], pp, xx[:], T.SL[:], False, True, n=C, cy=4.0)
        ts([(b, "p")], [fk("u")], sf("u"), pp, MAG, ALU.add, -MAG, ALU.add)
        tt([(b, "p"), fk("u")], [hk(L)], sh(L), pp, sf("u"), ALU.subtract, cy=1.0)
        ts([fk("u")], [hk(R)], sh(R), sf("u"), 1.0 / 4096, ALU.mult)
        if t < 3:
            j = slot[("SH", h)][L] * C; i = slot[("SU", h)][L] * C
            ts([hk(L), hk(R)], [uk(L), uk(R)], T["SU_%d" % h][:, i:i + 2 * C], T["SH_%d" % h][:, j:j + 2 * C], float(CTR), ALU.add, n=64)

    def expand(h, ep, t):
        decode(h, t)
        su, uk = view("SU", h); sc, sk = view("SC", h); sh, hk = view("SH", h); sb, bk_ = view("SB", h)
        o = 2 + h
        if t == 1:
            votes(ep, h, [(su("L1"), uk("L1")), (su("R1"), uk("R1"))], NV2, ("R1", "L1"))
        else:
            y = B[o][:, 448:512]; dg = T["DG_%d" % h]
            mm([("DG", h, "q1"), hk("L1")], [(o, "xc")], y, dg[:, 128:256], sh("L1"), True, False, n=C)
            mm([("DG", h, "q0"), hk("R1")], [(o, "xc")], y, dg[:, 0:128], sh("R1"), False, False, n=C)
            ts([hk("L2")], [bk_("qe")], sb("qe"), sh("L2"), float(Z - CTR), ALU.is_ge, 8192.0, ALU.mult)
            mm(["IB", bk_("qe")], [(o, "xc")], y, T.IB[:], sb("qe"), False, True, n=C)
            ts([(o, "xc")], [uk("C")], su("C"), y, float(Z - CTR), ALU.min, float(CTR), ALU.add)
            ts([(o, "xc")], [hk("C")], sh("C"), y, float(Z - CTR), ALU.min)
            votes(ep, h, [(su("L2"), uk("L2")), (su("R2"), uk("R2")), (su("C"), uk("C"))], NV3, ("R2", "L2"))

    def last(h, ep):
        decode(h, 3)
        sh, hk = view("SH", h); sb, bk_ = view("SB", h)
        ts([hk("L3")], [bk_("live")], sb("live"), sh("L3"), float(Z - CTR), ALU.is_lt)
        for kb in range(KN // 4):
            P = (6 if h == 0 else 0) + kb
            for kl in range(4):
                k = 4 * kb + kl
                for mp in range(H):
                    i = mp * KN + k
                    mm([("LR", i), bk_("live")], [(P, "lv")], B[P][:, 128 * kl + mp:128 * kl + 128:H], T.LR[:, 128 * i:128 * i + 128], sb("live"), n=C)
            b = (h * KN) // 4 + kb
            cp([(P, "lv")], [("lv", b)], T.LV[:, 512 * b:512 * b + 512], B[P][:], 512)

    def lookups(h, ep):
        su, uk = view("SU", h); sb, bk_ = view("SB", h)
        lk = [("lv", j) for j in range(4)] + [("lvz",)]
        b = 4 + h; die = B[b][:, 320:320 + C]
        for j, (n, l) in enumerate((("GA", "x2"), ("GB", "x3"))):
            for c in range(0, NP, CP):
                cp(lk + [uk(l)], [(n, h, c)], T["%s_%d" % (n, h)][:, c:c + CP], T.LV[:, 0:WW].indirect(su(l)[:, c // 16:(c + CP) // 16]), CP, CG)
        mm(["I4", bk_("live")], [(b, "die")], die, T.I4[:], sb("live"), True, False, n=C)
        for n in ("e2", "e3"): mm(["NI", bk_(n)], [(b, "die")], die, T.NI[:], sb(n), False, False, n=C)
        for j, n in enumerate(("GA", "GB")):
            for i in range(16):
                mm([("FD", i)] + [(n, h, c) for c in range(0, NP, CP)], [(b, "die")], die, T.FD[:, 128 * i:128 * i + 128], T["%s_%d" % (n, h)][:, i:NP:16], False, j == 1 and i == 15, n=C)

    def ab(h, ep):
        sh, hk = view("SH", h); o = 2 + h; dg = T["DG_%d" % h]
        for y, terms in ((384, (("n0", "L2", 4), ("n2", "C", 5), ("wL", "L3", 6))), (448, (("n3", "L2", 7), ("n5", "C", 8), ("n4", "R2", 9), ("bL", "L3", 10), ("bR", "R3", 11)))):
            for i, (c, l, j) in enumerate(terms):
                mm([("DG", h, "c" + c), hk(l)], [(o, "xc")], B[o][:, y:y + C], dg[:, 128 * j:128 * j + 128], sh(l), i == 0, i == len(terms) - 1, n=C)

    def calls(h, ep):
        sb, bk_ = view("SB", h); su, uk = view("SU", h); sh, hk = view("SH", h); o = 2 + h; b = 4 + h
        ts([(b, "die")], [bk_("go")], sb("go"), B[b][:, 320:320 + C], 4.0, ALU.is_equal)
        ts([(b, "die")], [bk_("ng")], sb("ng"), B[b][:, 320:320 + C], 4.0, ALU.not_equal)
        for n, y in (("ma", 384), ("mb", 448)): tt([(o, "xc"), bk_("go")], [hk(n)], sh(n), B[o][:, y:y + C], sb("go"), ALU.mult, cy=1.0)
        tt([("IV", h), bk_("ng")], [hk("nv")], sh("nv"), T.IV[:, C * h:C * h + C], sb("ng"), ALU.mult)
        for n, y in (("ma", 0), ("mb", 64)):
            mm(["IB", hk("nv")], [(b, "ab")], B[b][:, y:y + C], T.IB[:], sh("nv"), True, False, n=C)
            mm(["IB", hk(n)], [(b, "ab")], B[b][:, y:y + C], T.IB[:], sh(n), False, True, n=C)
        i = slot[("SU", h)]["a"] * C
        ts([(b, "ab")], [uk("a"), uk("b")], T["SU_%d" % h][:, i:i + 2 * C], B[b][:, 0:128], float(CTR), ALU.add, n=128)

    def neww(h, ep):
        t = T["W%d" % ep]
        su, uk = view("SU", h)
        wk = [("w", ep, j) for j in range(4)] + [("wg", ep), ("wz", ep)]
        for c in range(0, NP, CP):
            for n, l in (("GA", "a"), ("GB", "b")):
                cp(wk + [uk(l)], [(n, h, c)], T["%s_%d" % (n, h)][:, c:c + CP], t[:, 0:WW].indirect(su(l)[:, c // 16:(c + CP) // 16]), CP, CG)

    def listw(h):
        for j, c in enumerate(range(0, NP, 512)):
            P = (6 if h == 0 else 0) + j
            mm(["IB", "QT"], [(P, "nw")], B[P][:], T.IB[:], T.QT[:], True, False, n=512)
            for n in ("GA", "GB"): mm(["HB", (n, h, c)], [(P, "nw")], B[P][:], T.HB[:], T["%s_%d" % (n, h)][:, c:c + 512], False, n == "GB", n=512)
            ts([(P, "nw")], [("WP", h, j)], T.WP[:, h * NP + c:h * NP + c + 512], B[P][:], 8388608.0, ALU.add, -8388608.0, ALU.add, n=512)

    def classw(h):
        for kb in range(KN // 4):
            P = (6 if h == 0 else 2) + kb
            for kl in range(4):
                mm(["IB"] + [("WP", h, j) for j in range(NP // 512)], [(P, "cw")], B[P][:, 128 * kl:128 * kl + 128], T.IB[:], T.WP[:, h * NP + 4 * kb + kl:h * NP + NP:KN])
            b = h * KN // 4 + kb
            cp([(P, "cw")], [("w", 2, b)], T.W2[:, 512 * b:512 * b + 512], B[P][:], 512)

    def outw(h):
        for kb in range(KN // 4):
            P = (6 if h == 0 else 0) + kb
            mm(["IB", "QT"], [(P, "nw")], B[P][:], T.IB[:], T.QT[:], True, False, n=512)
            for n in ("GA", "GB"):
                for kl in range(4):
                    mm(["HB"] + [(n, h, c) for c in range(0, NP, CP)], [(P, "nw")], B[P][:, 128 * kl:128 * kl + 128], T.HB[:], T["%s_%d" % (n, h)][:, 4 * kb + kl:NP:KN], False, n == "GB" and kl == 3)
            b = h * KN // 4 + kb
            ts([(P, "nw")], [("w", 1, b)], T.W1[:, 512 * b:512 * b + 512], B[P][:], 8388608.0, ALU.add, -8388608.0, ALU.add, n=512)
            dma("Y", [("w", 1, b)], [("yw", b)], T.yw[:, 512 * b:512 * b + 512], T.W1[:, 512 * b:512 * b + 512])

    def kidsout(h, ep, kb):
        sb, bk_ = view("SB", h); sh, hk = view("SH", h)
        b = h * KN // 4 + kb
        Pn, Pv = (6 + b % 2, b % 2) if ep == 1 else ((2, 3), (4, 5))[b % 2]
        todo = [(4 * kb + kl, kl, mp) for kl in range(4) for mp in range(H)]
        for j, (k, kl, mp) in enumerate(todo):
            i = mp * KN + k
            mm([("LR", i), bk_("ng")], [(Pn, "ng")], B[Pn][:, 128 * kl + mp:128 * kl + 128:H], T.LR[:, 128 * i:128 * i + 128], sb("ng"), n=C)
        if ep == 2: mm(["A0", "ON"], [(Pv, "vl")], B[Pv][:], T.A0[:], T.ON[:], True, False, n=512)
        for j, (k, kl, mp) in enumerate(todo):
            i = mp * KN + k
            for n, m in enumerate(("LR", "LB")):
                mm([(m, i), hk(("ma", "mb")[n])], [(Pv, "vl")], B[Pv][:, 128 * kl + mp:128 * kl + 128:H], T[m][:, 128 * i:128 * i + 128], sh(("ma", "mb")[n]),
                   ep == 1 and n == 0, n == 1 if ep == 1 else (n == 1 and j == len(todo) - 1), n=C)
        kf = T.KF[:, 512 * b:512 * b + 512]
        tt([("kf", b), (Pn, "ng")], [("kf", b)], kf, kf, B[Pn][:], ALU.mult, n=512, cy=1.0)
        tt([("kf", b), (Pv, "vl")], [("kf", b)], kf, kf, B[Pv][:], ALU.add, n=512, cy=1.0)
        if ep == 1:
            act([("w", 2, b)], [("PR", b)], T.PR[:, 512 * b:512 * b + 512], T.W2[:, 512 * b:512 * b + 512], ACT.Sign, n=512)
            mm(["AS", "ON"], [(Pn, "ab")], B[Pn][:], T.AS[:], T.ON[:], True, False, n=512)
            mm(["NB", ("PR", b)], [(Pn, "ab")], B[Pn][:], T.NB[:], T.PR[:, 512 * b:512 * b + 512], False, True, n=512)
            tt([("kf", b), (Pn, "ab")], [("kt", b)], T.KT[:, 512 * b:512 * b + 512], kf, B[Pn][:], ALU.add, n=512, cy=1.0)
        else: dma("Y", [("kf", b)], [("yk", b)], T.yk[:, 512 * b:512 * b + 512], kf)

    def absent(ep, b, P):
        t = T["W%d" % ep]
        wk = ("w", ep, b) if b < 4 else ("wg", ep)
        mm(["IB", "BT"], [(P, "ab")], B[P][:], T.IB[:], T.BT[:], True, False, n=512)
        mm(["NB", wk], [(P, "ab")], B[P][:], T.NB[:], t[:, 512 * b:512 * b + 512], False, True, n=512)
        if b < 4: tt([("ki", b), (P, "ab")], [("kt", b)], T.KT[:, 512 * b:512 * b + 512], T.KI[:, 512 * b:512 * b + 512], B[P][:], ALU.max, n=512, cy=1.0)
        else: tt(["GI", (P, "ab")], [("ktg", b)], T.KT[:, 512 * b:512 * b + 512], T.GI[:, 512 * b - V:512 * b - V + 512], B[P][:], ALU.max, n=512, cy=1.0)

    HS = range(H)

    def each(f, *a):
        for h in HS:
            half[0] = h
            f(h, *a)
        half[0] = None

    def start(h):
        positions(h)
        vote1(h)
    each(start)
    for b in range(4): absent(1, b, 4 + b % 2)
    for b in range(4): ts([("ki", b)], [("kf", b)], T.KF[:, 512 * b:512 * b + 512], T.KI[:, 512 * b:512 * b + 512], -4097.0 * CTR, ALU.add, n=512)
    for i in range(16):
        lin([("LR", i)], [("LB", i)], T.LB[:, 128 * i:128 * i + 128], T.LR[:, 128 * i:128 * i + 128], 4096.0, n=128)
    pp = {}

    def vote(h, ep, t): pp[h] = choose(h, ep, t)

    def table(h, ep):
        for kb in range(KN // 4): kidsout(h, ep, kb)

    def looks(h, ep):
        ab(h, ep)
        lookups(h, ep)

    def finish(h, ep):
        calls(h, ep)
        neww(h, ep)
        if ep == 1:
            listw(h)
            vote1(h)
            classw(h)
            if h == 0: ghosts(2)
    for ep in (1, 2):
        if ep == 2: each(table, 1)
        each(vote, ep, 1)
        for b in range(4, 7): absent(ep, b, 6 + b % 2)
        each(expand, ep, 1)
        each(vote, ep, 2)
        each(lambda h: drops(h, 2, pp[h]))
        each(expand, ep, 2)
        each(vote, ep, 3)
        each(lambda h: drops(h, 3, pp[h]))
        each(last, ep)
        each(looks, ep)
        each(finish, ep)
        if ep == 2:
            each(table, 2)
            each(outw)

    n = len(nodes); pred = [set() for _ in range(n)]
    lw = {}; lr = {}; bp = {}
    for i, (q, R, W, _e, _c, _l, _h) in enumerate(nodes):
        for k in R:
            if k in lw: pred[i].add(lw[k])
        for k in W:
            if k in lw: pred[i].add(lw[k])
            pred[i].update(lr.get(k, ()))
        for k in R + W:
            if bk(k) is not None:
                e = bp.setdefault(bk(k), {})
                for q2, j in e.items():
                    if q2 != q or q == "P": pred[i].add(j)
        for k in R + W:
            if bk(k) is not None: bp[bk(k)][q] = i
        for k in R: lr.setdefault(k, []).append(i)
        for k in W: lw[k] = i; lr[k] = []
    succ = [[] for _ in range(n)]
    for i in range(n):
        pred[i].discard(i)
        for j in pred[i]: succ[j].append(i)
    prio = [0.0] * n
    for i in range(n - 1, -1, -1):
        m = max([prio[j] for j in succ[i]] or [0.0])
        prio[i] = nodes[i][4] + nodes[i][5] + m + (WAKE if nodes[i][0] != "P" else 0.0)
    for i in range(n):
        if nodes[i][6] == 0: prio[i] += LEAD
    left = [len(p) for p in pred]; est = [0.0] * n; ready = {q: [] for q in eng}; free = {q: 0.0 for q in eng}; order = []

    def offer(i):
        for q in nodes[i][0]: ready[q].append(i)
    for i in range(n):
        if left[i] == 0: offer(i)
    while len(order) < n:
        best = None
        for q in ("S", "V", "P", "G", "Y"):
            if ready[q]:
                t0 = max(free[q], min(est[i] for i in ready[q]))
                if best is None or t0 < best[0]: best = (t0, q)
        t0, q = best
        i = max((i for i in ready[q] if est[i] <= t0 + 1e-9), key=lambda i: (prio[i], -i))
        for r in nodes[i][0]: ready[r].remove(i)
        free[q] = t0 + nodes[i][4]; order.append((i, q))
        for j in succ[i]:
            same = nodes[j][0] == q
            est[j] = max(est[j], free[q] + nodes[i][5] + ((0.0 if q == "P" else SELF) if same else WAKE))
            left[j] -= 1
            if left[j] == 0: offer(j)
    for i, q in order: nodes[i][3](q)
    for s in cnt:
        g.wait_ge(T.sem[s], cnt[s])
